import numpy as np, ml_dtypes
CORES = [7,391,135,263,15,399,143,271]
N = 8
NH, QP = 8, 32
def setup_inputs(rng):
    q = rng.standard_normal((N, 128, NH * QP), dtype=np.float32) / 4; k = rng.standard_normal((N, 128, NH * 128), dtype=np.float32)
    a = 2 * np.pi * rng.random((N, NH * QP)); s = 400 * rng.random((N, NH * QP)) ** 1.5; q[:, 0, :] = s * np.cos(a); q[:, 1, :] = s * np.sin(a); q[:, 2, :] = 150 * rng.standard_normal((N, NH * QP)); k[:, 2, :] = 1 + k[:, 2, :] / 50
    a = (2 * np.pi * rng.random((1, NH, 1)) + np.pi / 2 * (rng.permuted(np.tile(np.arange(N), (NH, 1)), axis=1).T.reshape(N, NH, 1) + 0.5) / N - 0.5 + rng.random((N, NH, 128))).reshape(N, NH * 128); k[:, 0, :] = np.cos(a); k[:, 1, :] = np.sin(a)
    return {"q": q.astype(ml_dtypes.bfloat16), "k": k.astype(ml_dtypes.bfloat16), "v": rng.standard_normal((N, 128, NH * 128), dtype=np.float32).astype(ml_dtypes.bfloat16)}
def setup_inputs_big(rng):
    d = setup_inputs(rng)
    for k in ("v",): d[k] = (d[k].astype(np.float32) * 1048576.0).astype(d[k].dtype)
    return d
def setup_inputs_small(rng):
    d = setup_inputs(rng)
    for k in ("v",): d[k] = (d[k].astype(np.float32) * (1 / 1048576.0)).astype(d[k].dtype)
    return d
def reference(q, k, v):
    Q, K, V = q.astype(np.float64), k.astype(np.float64), v.astype(np.float64)
    y = np.zeros((N, QP, NH * 128))
    for r in range(N):
        for h in range(NH):
            S = np.concatenate([K[j][:, 128 * h:128 * h + 128].T @ Q[r][:, QP * h:QP * h + QP] for j in range(N)], axis=0)
            P = np.exp(S - S.max(axis=0)); P = P / P.sum(axis=0)
            y[r][:, 128 * h:128 * h + 128] = P.T @ np.concatenate([V[j][:, 128 * h:128 * h + 128] for j in range(N)], axis=0)
    return {"y": y.astype(ml_dtypes.bfloat16)}

@@ -1,0 +1,278 @@
+from concourse.bass import DstId, RemoteDMATransfer
+from concourse.mybir import AluOpType, AxisListType, ActivationFunctionType
+
+N, NH, QP, KP = 8, 8, 32, 128
+W = QP + KP
+
+SCRATCH = {
+    "qk": ("sbuf", [128, NH, W], "bfloat16"),
+    "vs": ("sbuf", [128, NH * 128], "bfloat16"),
+    "qkl": ("sbuf", [128, N, W], "bfloat16"),
+    "vl": ("sbuf", [128, N * 128], "bfloat16"),
+    "rqk": ("sbuf", [128, 2, W], "bfloat16"),
+    "rv": ("sbuf", [128, 2 * 128], "bfloat16"),
+    "qc": ("sbuf", [128, 256], "bfloat16"),
+    "zero": ("sbuf", [128, 128], "bfloat16"),
+    "ones": ("sbuf", [128, 128], "bfloat16"),
+    "ident": ("sbuf", [128, 128], "bfloat16"),
+    "p": ("sbuf", [128, 2048], "bfloat16"),
+    "pts": ("sbuf", [128, 2048], "bfloat16"),
+    "st": ("sbuf", [128, 16], "float32"),
+    "yqx": ("sbuf", [128, 128], "bfloat16"),
+    "yl": ("sbuf", [128, NH * 128], "bfloat16"),
+    "sx": ("psum", [128, 1024], "float32"),
+    "sy": ("psum", [128, 1024], "float32"),
+    "pta": ("psum", [128, 1024], "bfloat16"),
+    "ptb": ("psum", [128, 1024], "bfloat16"),
+    "ox": ("psum", [128, 512], "float32"),
+    "oy": ("psum", [128, 512], "float32"),
+}
+
+_EV = ["q", "s0", "s1", "red", "nm", "exp0", "exp1", "t0", "t1", "c0", "c1", "o", "l", "rl", "f"]
+SEMAPHORES = (["ld_qk", "ld_v", "st_y", "snd", "zero", "ones", "id", "rq0", "rq1", "rv0", "rv1"]
+              + ["aqk%d" % j for j in range(N)] + ["av%d" % j for j in range(N)] + ["ay%d" % j for j in range(N)]
+              + ["%s_%d" % (e, b) for e in _EV for b in range(2)])
+
+
+def _bits(m):
+    return [b for b in range(16) if (m >> b) & 1]
+
+
+def _mk(bs):
+    m = 0
+    for b in bs:
+        m |= 1 << b
+    return m
+
+
+def _plan(T, topo):
+    C = [int(c) for c in T.cores]
+    R = range(len(C))
+    host = [topo.host(c) for c in C]
+    chip = [topo.chip(c) for c in C]
+
+    def ok(a, b):
+        return topo.may_write(C[a], C[b])
+
+    far = [[j for j in R if j != r and not ok(r, j)] for r in R]
+    near = [[j for j in R if j != r and ok(r, j)] for r in R]
+    peer = [[j for j in R if topo.same_plane(C[r], C[j])][0] for r in R]
+    colour = [0 if (host[r] == host[0] or not ok(0, r)) else 1 for r in R]
+    side = [0 if chip[r] == chip[0] else 1 for r in R]
+    slot = [2 * colour[r] + side[r] for r in R]
+    xs = [[j for j in R if host[j] in (host[far[w][0]], host[peer[w]])] for w in R]
+
+    def relay(s, d):
+        if chip[s] == chip[d]:
+            return peer[s]
+        return [m for m in R if chip[m] == chip[s] and host[m] != host[s] and m != peer[s] and ok(s, m) and ok(m, d)][0]
+
+    flows = [sorted((s, d) for s in R for d in far[s] if relay(s, d) == m) for m in R]
+    return dict(C=C, host=host, chip=chip, far=far, near=near, peer=peer, slot=slot, xs=xs, relay=relay, flows=flows)
+
+
+def rank_program(g, core, T, topo):
+    r = T.rank_of(core)
+    if r is None:
+        return
+    P = _plan(T, topo)
+    C, far, near, slot, xs, flows = P["C"], P["far"], P["near"], P["slot"], P["xs"], P["flows"]
+    R = range(N)
+    S = T.sem
+    EXP = ActivationFunctionType.Exp
+
+    def ev(name, b):
+        return S["%s_%d" % (name, b)]
+
+    m = 0xFFFF
+    for j in near[r]:
+        m &= topo.mask(core, C[j])
+    eng = _bits(m)
+    half = len(eng) // 2
+    two_hop = [eng[0:half // 2], eng[half // 2:half]]
+    single = [[e] for e in eng[half:]]
+
+    def groups(kind):
+        return single + [two_hop[kind]]
+
+    def n_direct(s, d, kind):
+        return len(groups(kind)[near[s].index(d)])
+
+    def n_in(s, kind):
+        return len(two_hop[0]) if r in far[s] else n_direct(s, r, kind)
+
+    sent = [0]
+
+    def tr(src, dst, dsts, sem, engs):
+        ids = []
+        for d in dsts:
+            rid, pid = topo.addr(C[d], core)
+            ids.append(DstId(rid=rid, pnc=pid))
+        sent[0] += len(engs)
+        return RemoteDMATransfer(dst_ids=ids, dma_engine_mask=_mk(engs), remote_sem=sem, srcs=[src],
+                                 dsts=[dst for _ in dsts], alu_op=0)
+
+    def vcol(t, j):
+        return t[:, 128 * j:128 * j + 128]
+
+    def q_of(j):
+        return T.qk[:, r, 0:QP] if j == r else T.qkl[:, j, 0:QP]
+
+    def k_of(j):
+        return T.qk[:, r, QP:W] if j == r else T.qkl[:, j, QP:W]
+
+    def v_of(j):
+        return vcol(T.vs, r) if j == r else vcol(T.vl, j)
+
+    blk = [0 if j in xs[r] else 1 for j in R]
+    ys = [j for j in R if blk[j] == 1 and j != r]
+    xnear = [j for j in xs[r] if j not in far[r]]
+    ko = [r] + ys + xnear + far[r]
+    SB, PT, OB = [T.sx, T.sy], [T.pta, T.ptb], [T.ox, T.oy]
+
+    g.sync.dma_start(T.qk[:, :, QP:W], T.k[:, :]).then_inc(S.ld_qk, 16)
+    g.scalar.dma_start(T.qk[:, :, 0:QP], T.q[:, :]).then_inc(S.ld_qk, 16)
+    g.sync.dma_start(T.vs[:, :], T.v[:, :]).then_inc(S.ld_v, 16)
+
+    g.wait_ge(S.ld_qk, 32)
+    call = []
+    for i, d in enumerate(far[r]):
+        mid = P["relay"](r, d)
+        sl = flows[mid].index((r, d))
+        call.append(tr(T.qk[:, d, :], T.rqk[:, sl, :], [mid], S["rq%d" % sl], two_hop[i]))
+    g.remote_dma_fused(call, local_sem=S.snd)
+    g.remote_dma_fused([tr(T.qk[:, d, :], T.qkl[:, r, :], [d], S["aqk%d" % r], groups(0)[i])
+                        for i, d in enumerate(near[r])], local_sem=S.snd)
+    g.wait_ge(S.ld_v, 16)
+    call = []
+    for i, d in enumerate(far[r]):
+        mid = P["relay"](r, d)
+        sl = flows[mid].index((r, d))
+        call.append(tr(vcol(T.vs, d), vcol(T.rv, sl), [mid], S["rv%d" % sl], two_hop[i]))
+    g.remote_dma_fused(call, local_sem=S.snd)
+    g.wait_ge(S.ones, 1)
+    g.affine_select(T.ident[:, :], T.ones[:, :], [[-1, 128]], AluOpType.is_equal, 0.0, 0, 1).then_inc(S.id, 1)
+    for sl in range(2):
+        g.wait_ge(S["rq%d" % sl], len(two_hop[0]))
+    g.remote_dma_fused([tr(T.rqk[:, sl, :], T.qkl[:, s, :], [d], S["aqk%d" % s], two_hop[sl])
+                        for sl, (s, d) in enumerate(flows[r])], local_sem=S.snd)
+    g.remote_dma_fused([tr(vcol(T.vs, d), vcol(T.vl, r), [d], S["av%d" % r], groups(1)[i])
+                        for i, d in enumerate(near[r])], local_sem=S.snd)
+    for sl in range(2):
+        g.wait_ge(S["rv%d" % sl], len(two_hop[0]))
+    g.remote_dma_fused([tr(vcol(T.rv, sl), vcol(T.vl, s), [d], S["av%d" % s], two_hop[sl])
+                        for sl, (s, d) in enumerate(flows[r])], local_sem=S.snd)
+    g.wait_ge(ev("f", 0), 1)
+    g.remote_dma_fused([tr(T.yqx[:, :], vcol(T.yl, r), xnear, S["ay%d" % r], eng)], local_sem=S.snd)
+    g.wait_ge(ev("f", 1), 1)
+    g.remote_dma_fused([tr(vcol(T.yl, r), vcol(T.yl, r), ys, S["ay%d" % r], eng)], local_sem=S.snd)
+    fw = [w for w in R if r in xs[w] and r not in far[w]]
+    call = []
+    for i, w in enumerate(fw):
+        g.wait_ge(S["ay%d" % w], len(eng))
+        d = [x for x in far[w] if P["chip"][x] == P["chip"][r]][0]
+        call.append(tr(vcol(T.yl, w), vcol(T.yl, w), [d], S["ay%d" % w], eng[i * half:(i + 1) * half]))
+    g.remote_dma_fused(call, local_sem=S.snd)
+    g.wait_ge(S.snd, sent[0])
+
+    a = g.scalar
+    a.wait_ge(S.zero, 1)
+    a.activation(T.ones[:, :], T.zero[:, :], EXP).then_inc(S.ones, 1)
+    for b in range(2):
+        a.wait_ge(ev("nm", b), 1)
+        for hf in range(2):
+            a.activation(T.p[:, 1024 * b + 512 * hf:1024 * b + 512 * hf + 512], SB[b][:, 512 * hf:512 * hf + 512], EXP,
+                         bias=T.st[:, 8 * b + 2:8 * b + 3], scale=1.0,
+                         accum_out=T.st[:, 8 * b + 3 + hf:8 * b + 4 + hf]).then_inc(ev("exp%d" % hf, b), 1)
+
+    pe = g.tensor
+
+    def score(b, kp):
+        pe.matmul(SB[b][:, 128 * kp:128 * kp + 128], T.qc[:, 128 * b:128 * b + 128], k_of(ko[kp]), True, True
+                  ).then_inc(ev("s%d" % (kp // 4), b), 1)
+
+    pe.wait_ge(S.ld_qk, 32)
+    pe.wait_ge(ev("q", 1), 4)
+    for kp in range(6):
+        if ko[kp] != r:
+            pe.wait_ge(S["aqk%d" % ko[kp]], n_in(ko[kp], 0))
+        score(1, kp)
+    pe.wait_ge(ev("q", 0), 4)
+    for kp in range(6, 8):
+        pe.wait_ge(S["aqk%d" % ko[kp]], n_in(ko[kp], 0))
+    for kp in range(8):
+        score(0, kp)
+    for kp in range(6, 8):
+        score(1, kp)
+    pe.wait_ge(S.id, 1)
+    pe.wait_ge(S.ld_v, 16)
+    for b in range(2):
+        for hf in range(2):
+            pe.wait_ge(ev("exp%d" % hf, b), 1)
+            for i in range(4):
+                kp = 4 * hf + i
+                pe.transpose(PT[hf][:, 512 * b + 128 * i:512 * b + 128 * i + 128],
+                             T.p[:, 1024 * b + 128 * kp:1024 * b + 128 * kp + 128], T.ident[:, :]
+                             ).then_inc(ev("t%d" % hf, b), 1)
+        for kp in range(8):
+            if kp % 4 == 0:
+                pe.wait_ge(ev("c%d" % (kp // 4), b), 1)
+            if b == 0 and ko[kp] != r:
+                pe.wait_ge(S["av%d" % ko[kp]], n_in(ko[kp], 1))
+            pe.matmul(OB[b][:, 0:128], T.pts[:, 1024 * b + 128 * kp:1024 * b + 128 * kp + 128], v_of(ko[kp]),
+                      kp == 0, kp == 7).then_inc(ev("o", b), 1)
+
+    v = g.vector
+    v.memset(T.zero[:, :], 0.0).then_inc(S.zero, 1)
+
+    def take_q(j):
+        if j == r:
+            v.wait_ge(S.ld_qk, 32)
+        else:
+            v.wait_ge(S["aqk%d" % j], n_in(j, 0))
+        c = 128 * blk[j] + QP * slot[j]
+        v.tensor_copy(T.qc[:, c:c + QP], q_of(j)).then_inc(ev("q", blk[j]), 1)
+
+    def neg_max(b, hf):
+        v.wait_ge(ev("s%d" % hf, b), 4)
+        v.tensor_reduce(T.st[:, 8 * b + hf:8 * b + hf + 1], SB[b][:, 512 * hf:512 * hf + 512], axis=AxisListType.X,
+                        op=AluOpType.max, negate=True).then_inc(ev("red", b), 1)
+
+    def join_max(b):
+        v.wait_ge(ev("red", b), 2)
+        v.tensor_tensor(T.st[:, 8 * b + 2:8 * b + 3], T.st[:, 8 * b:8 * b + 1], T.st[:, 8 * b + 1:8 * b + 2],
+                        AluOpType.min).then_inc(ev("nm", b), 1)
+
+    for j in [r] + ys + xnear:
+        take_q(j)
+    neg_max(1, 0)
+    for j in far[r]:
+        take_q(j)
+    neg_max(0, 0)
+    neg_max(0, 1)
+    join_max(0)
+    neg_max(1, 1)
+    join_max(1)
+    for b in range(2):
+        for hf in range(2):
+            v.wait_ge(ev("t%d" % hf, b), 4)
+            v.tensor_copy(T.pts[:, 1024 * b + 512 * hf:1024 * b + 512 * hf + 512],
+                          PT[hf][:, 512 * b:512 * b + 512]).then_inc(ev("c%d" % hf, b), 1)
+            if hf == 0:
+                v.wait_ge(ev("exp0", b), 1)
+                v.wait_ge(ev("exp1", b), 1)
+                v.tensor_tensor(T.st[:, 8 * b + 5:8 * b + 6], T.st[:, 8 * b + 3:8 * b + 4], T.st[:, 8 * b + 4:8 * b + 5],
+                                AluOpType.add).then_inc(ev("l", b), 1)
+                v.wait_ge(ev("l", b), 1)
+                v.reciprocal(T.st[:, 8 * b + 6:8 * b + 7], T.st[:, 8 * b + 5:8 * b + 6]).then_inc(ev("rl", b), 1)
+        v.wait_ge(ev("o", b), 8)
+        v.wait_ge(ev("rl", b), 1)
+        v.tensor_scalar(T.yqx[:, :] if b == 0 else vcol(T.yl, r), OB[b][:, 0:128], T.st[:, 8 * b + 6:8 * b + 7], None,
+                        AluOpType.mult).then_inc(ev("f", b), 1)
+
+    for w in R:
+        if w != r:
+            g.sync.wait_ge(S["ay%d" % w], half if r in far[w] else len(eng))
+    g.sync.wait_ge(ev("f", 1), 1)
+    g.sync.dma_start(T.y[:, :], T.yl[QP * slot[r]:QP * slot[r] + QP, :]).then_inc(S.st_y, 16)
+    g.sync.wait_ge(S.st_y, 16)

@@ -2,36 +2,49 @@ from concourse.bass import DstId, RemoteDMATransfer
 from concourse.mybir import AluOpType, AxisListType, ActivationFunctionType
 
 N, NH, QP, KP = 8, 8, 32, 128
-W = QP + KP
+G = 4
+VW = 272
+PW = 2 * 129 + 2
+POS = [129, 0]
+OCOL = [130, 0]
 
 SCRATCH = {
-    "qk": ("sbuf", [128, NH, W], "bfloat16"),
+    "qs": ("sbuf", [128, NH * QP], "bfloat16"),
+    "ks": ("sbuf", [128, NH * KP], "bfloat16"),
     "vs": ("sbuf", [128, NH * 128], "bfloat16"),
-    "qkl": ("sbuf", [128, N, W], "bfloat16"),
-    "vl": ("sbuf", [128, N * 128], "bfloat16"),
-    "rqk": ("sbuf", [128, 2, W], "bfloat16"),
-    "rv": ("sbuf", [128, 2 * 128], "bfloat16"),
-    "qc": ("sbuf", [128, 256], "bfloat16"),
+    "ql": ("sbuf", [128, 512], "bfloat16"),
+    "kl": ("sbuf", [128, G, 256], "bfloat16"),
+    "vl": ("sbuf", [128, G, VW], "bfloat16"),
     "zero": ("sbuf", [128, 128], "bfloat16"),
     "ones": ("sbuf", [128, 128], "bfloat16"),
     "ident": ("sbuf", [128, 128], "bfloat16"),
     "p": ("sbuf", [128, 2048], "bfloat16"),
     "pts": ("sbuf", [128, 2048], "bfloat16"),
-    "st": ("sbuf", [128, 16], "float32"),
-    "yqx": ("sbuf", [128, 128], "bfloat16"),
+    "nmy": ("sbuf", [128, 2], "bfloat16"),
+    "xs": ("sbuf", [128, PW], "bfloat16"),
+    "xl": ("sbuf", [128, PW], "bfloat16"),
+    "dl": ("sbuf", [128, 2], "float32"),
+    "dd": ("sbuf", [128, 4], "float32"),
+    "aa": ("sbuf", [128, 4], "float32"),
+    "t2": ("sbuf", [128, 258], "float32"),
+    "sm": ("sbuf", [128, 258], "float32"),
+    "rc": ("sbuf", [128, 2], "float32"),
     "yl": ("sbuf", [128, NH * 128], "bfloat16"),
-    "sx": ("psum", [128, 1024], "float32"),
-    "sy": ("psum", [128, 1024], "float32"),
+    "s0": ("psum", [128, 512], "float32"),
+    "s1": ("psum", [128, 512], "float32"),
+    "s2": ("psum", [128, 512], "float32"),
+    "s3": ("psum", [128, 512], "float32"),
     "pta": ("psum", [128, 1024], "bfloat16"),
     "ptb": ("psum", [128, 1024], "bfloat16"),
-    "ox": ("psum", [128, 512], "float32"),
-    "oy": ("psum", [128, 512], "float32"),
+    "oa": ("psum", [128, 512], "float32"),
+    "ob": ("psum", [128, 512], "float32"),
 }
 
-_EV = ["q", "s0", "s1", "red", "nm", "exp0", "exp1", "t0", "t1", "c0", "c1", "o", "l", "rl", "f"]
-SEMAPHORES = (["ld_qk", "ld_v", "st_y", "snd", "zero", "ones", "id", "rq0", "rq1", "rv0", "rv1"]
-              + ["aqk%d" % j for j in range(N)] + ["av%d" % j for j in range(N)] + ["ay%d" % j for j in range(N)]
-              + ["%s_%d" % (e, b) for e in _EV for b in range(2)])
+SEMAPHORES = (["ld_q", "ld_k", "ld_v", "ld_qo", "ld_vo", "st_y", "snd", "zero", "ones", "id", "onec",
+               "aq", "aqx", "axl", "m1", "m2", "m3", "m7"]
+              + ["ak%d" % s for s in range(G)] + ["av%d" % s for s in range(G)] + ["ay%d" % s for s in range(G)]
+              + ["%s%d" % (e, u) for e in ("s_", "nm_", "e_", "t_", "c_", "o_") for u in range(4)]
+              + ["%s%d" % (e, i) for e in ("fx", "fy", "m4_", "m5_", "m6_") for i in range(2)])
 
 
 def _bits(m):
@@ -48,27 +61,13 @@ def _mk(bs):
 def _plan(T, topo):
     C = [int(c) for c in T.cores]
     R = range(len(C))
-    host = [topo.host(c) for c in C]
+    rack = [topo.rack(topo.host(c)) for c in C]
     chip = [topo.chip(c) for c in C]
-
-    def ok(a, b):
-        return topo.may_write(C[a], C[b])
-
-    far = [[j for j in R if j != r and not ok(r, j)] for r in R]
-    near = [[j for j in R if j != r and ok(r, j)] for r in R]
-    peer = [[j for j in R if topo.same_plane(C[r], C[j])][0] for r in R]
-    colour = [0 if (host[r] == host[0] or not ok(0, r)) else 1 for r in R]
-    side = [0 if chip[r] == chip[0] else 1 for r in R]
-    slot = [2 * colour[r] + side[r] for r in R]
-    xs = [[j for j in R if host[j] in (host[far[w][0]], host[peer[w]])] for w in R]
-
-    def relay(s, d):
-        if chip[s] == chip[d]:
-            return peer[s]
-        return [m for m in R if chip[m] == chip[s] and host[m] != host[s] and m != peer[s] and ok(s, m) and ok(m, d)][0]
-
-    flows = [sorted((s, d) for s in R for d in far[s] if relay(s, d) == m) for m in R]
-    return dict(C=C, host=host, chip=chip, far=far, near=near, peer=peer, slot=slot, xs=xs, relay=relay, flows=flows)
+    partner = [[j for j in R if rack[j] != rack[r] and chip[j] == chip[r] and topo.may_write(C[r], C[j])][0] for r in R]
+    base = [j for j in R if rack[j] == rack[0]]
+    idx = [base.index(j) if j in base else base.index(partner[j]) for j in R]
+    grp = [[j for j in R if rack[j] == rack[r]] for r in R]
+    return dict(C=C, partner=partner, idx=idx, grp=grp)
 
 
 def rank_program(g, core, T, topo):
@@ -76,30 +75,21 @@ def rank_program(g, core, T, topo):
     if r is None:
         return
     P = _plan(T, topo)
-    C, far, near, slot, xs, flows = P["C"], P["far"], P["near"], P["slot"], P["xs"], P["flows"]
-    R = range(N)
+    C, idx = P["C"], P["idx"]
+    me = idx[r]
+    mate = P["partner"][r]
+    others = [j for j in P["grp"][r] if j != r]
     S = T.sem
     EXP = ActivationFunctionType.Exp
-
-    def ev(name, b):
-        return S["%s_%d" % (name, b)]
+    CPY = ActivationFunctionType.Copy
 
     m = 0xFFFF
-    for j in near[r]:
+    for j in others + [mate]:
         m &= topo.mask(core, C[j])
     eng = _bits(m)
-    half = len(eng) // 2
-    two_hop = [eng[0:half // 2], eng[half // 2:half]]
-    single = [[e] for e in eng[half:]]
-
-    def groups(kind):
-        return single + [two_hop[kind]]
-
-    def n_direct(s, d, kind):
-        return len(groups(kind)[near[s].index(d)])
-
-    def n_in(s, kind):
-        return len(two_hop[0]) if r in far[s] else n_direct(s, r, kind)
+    per = len(eng) // (len(others) + 1)
+    lane = [eng[per * t:per * t + per] for t in range(len(others) + 1)]
+    cable = lane[len(others)]
 
     sent = [0]
 
@@ -112,167 +102,166 @@ def rank_program(g, core, T, topo):
         return RemoteDMATransfer(dst_ids=ids, dma_engine_mask=_mk(engs), remote_sem=sem, srcs=[src],
                                  dsts=[dst for _ in dsts], alu_op=0)
 
-    def vcol(t, j):
-        return t[:, 128 * j:128 * j + 128]
+    def k_of(s, i):
+        return T.ks[:, 256 * me + 128 * i:256 * me + 128 * i + 128] if s == me else T.kl[:, s, 128 * i:128 * i + 128]
 
-    def q_of(j):
-        return T.qk[:, r, 0:QP] if j == r else T.qkl[:, j, 0:QP]
+    def v_of(s, i):
+        return T.vl[:, s, 7:136] if i == 0 else T.vl[:, s, 136:265]
 
-    def k_of(j):
-        return T.qk[:, r, QP:W] if j == r else T.qkl[:, j, QP:W]
+    ko = [me] + [idx[j] for j in others]
+    SB, PT, OB = [T.s0, T.s1, T.s2, T.s3], [T.pta, T.ptb], [T.oa, T.ob]
 
-    def v_of(j):
-        return vcol(T.vs, r) if j == r else vcol(T.vl, j)
-
-    blk = [0 if j in xs[r] else 1 for j in R]
-    ys = [j for j in R if blk[j] == 1 and j != r]
-    xnear = [j for j in xs[r] if j not in far[r]]
-    ko = [r] + ys + xnear + far[r]
-    SB, PT, OB = [T.sx, T.sy], [T.pta, T.ptb], [T.ox, T.oy]
-
-    g.sync.dma_start(T.qk[:, :, QP:W], T.k[:, :]).then_inc(S.ld_qk, 16)
-    g.scalar.dma_start(T.qk[:, :, 0:QP], T.q[:, :]).then_inc(S.ld_qk, 16)
+    g.scalar.dma_start(T.qs[:, :], T.q[:, :]).then_inc(S.ld_q, 16)
+    g.sync.dma_start(T.ks[:, :], T.k[:, :]).then_inc(S.ld_k, 16)
+    for i in range(2):
+        h = 2 * me + i
+        g.scalar.dma_start(T.ql[:, 128 * i + QP * me:128 * i + QP * me + QP], T.q[:, QP * h:QP * h + QP]).then_inc(S.ld_qo, 16)
     g.sync.dma_start(T.vs[:, :], T.v[:, :]).then_inc(S.ld_v, 16)
+    g.scalar.dma_start(T.vl[:, me, 8:264], T.v[:, 256 * me:256 * me + 256]).then_inc(S.ld_vo, 16)
 
-    g.wait_ge(S.ld_qk, 32)
+    g.wait_ge(S.ld_q, 16)
     call = []
-    for i, d in enumerate(far[r]):
-        mid = P["relay"](r, d)
-        sl = flows[mid].index((r, d))
-        call.append(tr(T.qk[:, d, :], T.rqk[:, sl, :], [mid], S["rq%d" % sl], two_hop[i]))
-    g.remote_dma_fused(call, local_sem=S.snd)
-    g.remote_dma_fused([tr(T.qk[:, d, :], T.qkl[:, r, :], [d], S["aqk%d" % r], groups(0)[i])
-                        for i, d in enumerate(near[r])], local_sem=S.snd)
-    g.wait_ge(S.ld_v, 16)
-    call = []
-    for i, d in enumerate(far[r]):
-        mid = P["relay"](r, d)
-        sl = flows[mid].index((r, d))
-        call.append(tr(vcol(T.vs, d), vcol(T.rv, sl), [mid], S["rv%d" % sl], two_hop[i]))
+    for t, d in enumerate(others):
+        for i in range(2):
+            h = 2 * idx[d] + i
+            call.append(tr(T.qs[:, QP * h:QP * h + QP], T.ql[:, 128 * i + QP * me:128 * i + QP * me + QP], [d], S.aq,
+                           [lane[t][i]]))
     g.remote_dma_fused(call, local_sem=S.snd)
     g.wait_ge(S.ones, 1)
     g.affine_select(T.ident[:, :], T.ones[:, :], [[-1, 128]], AluOpType.is_equal, 0.0, 0, 1).then_inc(S.id, 1)
-    for sl in range(2):
-        g.wait_ge(S["rq%d" % sl], len(two_hop[0]))
-    g.remote_dma_fused([tr(T.rqk[:, sl, :], T.qkl[:, s, :], [d], S["aqk%d" % s], two_hop[sl])
-                        for sl, (s, d) in enumerate(flows[r])], local_sem=S.snd)
-    g.remote_dma_fused([tr(vcol(T.vs, d), vcol(T.vl, r), [d], S["av%d" % r], groups(1)[i])
-                        for i, d in enumerate(near[r])], local_sem=S.snd)
-    for sl in range(2):
-        g.wait_ge(S["rv%d" % sl], len(two_hop[0]))
-    g.remote_dma_fused([tr(vcol(T.rv, sl), vcol(T.vl, s), [d], S["av%d" % s], two_hop[sl])
-                        for sl, (s, d) in enumerate(flows[r])], local_sem=S.snd)
-    g.wait_ge(ev("f", 0), 1)
-    g.remote_dma_fused([tr(T.yqx[:, :], vcol(T.yl, r), xnear, S["ay%d" % r], eng)], local_sem=S.snd)
-    g.wait_ge(ev("f", 1), 1)
-    g.remote_dma_fused([tr(vcol(T.yl, r), vcol(T.yl, r), ys, S["ay%d" % r], eng)], local_sem=S.snd)
-    fw = [w for w in R if r in xs[w] and r not in far[w]]
-    call = []
-    for i, w in enumerate(fw):
-        g.wait_ge(S["ay%d" % w], len(eng))
-        d = [x for x in far[w] if P["chip"][x] == P["chip"][r]][0]
-        call.append(tr(vcol(T.yl, w), vcol(T.yl, w), [d], S["ay%d" % w], eng[i * half:(i + 1) * half]))
-    g.remote_dma_fused(call, local_sem=S.snd)
+    g.wait_ge(S.ld_k, 16)
+    g.remote_dma_fused([tr(T.ks[:, 256 * idx[d]:256 * idx[d] + 256], T.kl[:, me, :], [d], S["ak%d" % me], lane[t])
+                        for t, d in enumerate(others)], local_sem=S.snd)
+    g.wait_ge(S.ld_v, 16)
+    g.remote_dma_fused([tr(T.vs[:, 256 * idx[d]:256 * idx[d] + 256], T.vl[:, me, 8:264], [d], S["av%d" % me], lane[t])
+                        for t, d in enumerate(others)], local_sem=S.snd)
+    g.wait_ge(S.ld_qo, 32)
+    g.wait_ge(S.aq, 2 * len(others))
+    g.remote_dma_fused([tr(T.ql[:, 0:256], T.ql[:, 256:512], [mate], S.aqx, cable)], local_sem=S.snd)
+    for i in range(2):
+        g.wait_ge(S["nm_%d" % (2 + i)], 1)
+        g.wait_ge(S["fx%d" % i], 1)
+    g.remote_dma_fused([tr(T.xs[:, :], T.xl[:, :], [mate], S.axl, eng)], local_sem=S.snd)
+    for i in range(2):
+        g.wait_ge(S["fy%d" % i], 1)
+    g.remote_dma_fused([tr(T.yl[:, 256 * me:256 * me + 256], T.yl[:, 256 * me:256 * me + 256], others, S["ay%d" % me], eng)],
+                       local_sem=S.snd)
     g.wait_ge(S.snd, sent[0])
 
     a = g.scalar
     a.wait_ge(S.zero, 1)
     a.activation(T.ones[:, :], T.zero[:, :], EXP).then_inc(S.ones, 1)
-    for b in range(2):
-        a.wait_ge(ev("nm", b), 1)
-        for hf in range(2):
-            a.activation(T.p[:, 1024 * b + 512 * hf:1024 * b + 512 * hf + 512], SB[b][:, 512 * hf:512 * hf + 512], EXP,
-                         bias=T.st[:, 8 * b + 2:8 * b + 3], scale=1.0,
-                         accum_out=T.st[:, 8 * b + 3 + hf:8 * b + 4 + hf]).then_inc(ev("exp%d" % hf, b), 1)
+
+    def shift_col(u):
+        return T.nmy[:, u:u + 1] if u < 2 else T.xs[:, 258 + u - 2:258 + u - 1]
+
+    for u in range(4):
+        a.wait_ge(S["nm_%d" % u], 1)
+        a.activation(T.p[:, 512 * u:512 * u + 512], SB[u][:, :], EXP, bias=shift_col(u), scale=1.0).then_inc(S["e_%d" % u], 1)
+    a.wait_ge(S.m2, 2)
+    a.activation(T.aa[:, :], T.dd[:, :], EXP).then_inc(S.m3, 1)
+    a.wait_ge(S.m3, 1)
+    for i in range(2):
+        a.wait_ge(S["o_%d" % i], 4)
+        a.activation(OB[i][:, 0:129], OB[i][:, 0:129], CPY, scale=T.aa[:, i:i + 1]).then_inc(S["m4_%d" % i], 1)
+    a.wait_ge(S.m7, 1)
+    a.activation(T.yl[:, 256 * me + 128:256 * me + 256], T.sm[:, OCOL[1]:OCOL[1] + 128], CPY,
+                 scale=T.rc[:, 0:1]).then_inc(S.fy1, 1)
 
     pe = g.tensor
 
-    def score(b, kp):
-        pe.matmul(SB[b][:, 128 * kp:128 * kp + 128], T.qc[:, 128 * b:128 * b + 128], k_of(ko[kp]), True, True
-                  ).then_inc(ev("s%d" % (kp // 4), b), 1)
+    def scores(u, first):
+        b, i = u // 2, u % 2
+        for kp, s in enumerate(ko):
+            if first and s != me:
+                pe.wait_ge(S["ak%d" % s], per)
+            pe.matmul(SB[u][:, 128 * kp:128 * kp + 128], T.ql[:, 256 * b + 128 * i:256 * b + 128 * i + 128], k_of(s, i),
+                      True, True).then_inc(S["s_%d" % u], 1)
 
-    pe.wait_ge(S.ld_qk, 32)
-    pe.wait_ge(ev("q", 1), 4)
-    for kp in range(6):
-        if ko[kp] != r:
-            pe.wait_ge(S["aqk%d" % ko[kp]], n_in(ko[kp], 0))
-        score(1, kp)
-    pe.wait_ge(ev("q", 0), 4)
-    for kp in range(6, 8):
-        pe.wait_ge(S["aqk%d" % ko[kp]], n_in(ko[kp], 0))
-    for kp in range(8):
-        score(0, kp)
-    for kp in range(6, 8):
-        score(1, kp)
+    def turn(u):
+        pe.wait_ge(S["e_%d" % u], 1)
+        for kp in range(G):
+            pe.transpose(PT[u % 2][:, 128 * kp:128 * kp + 128], T.p[:, 512 * u + 128 * kp:512 * u + 128 * kp + 128],
+                         T.ident[:, :]).then_inc(S["t_%d" % u], 1)
+
+    def pv(u, first):
+        i = u % 2
+        pe.wait_ge(S["c_%d" % u], 1)
+        if u < 2:
+            pe.wait_ge(S["fx%d" % i], 1)
+        for kp, s in enumerate(ko):
+            if first and s != me:
+                pe.wait_ge(S["av%d" % s], per)
+            pe.matmul(OB[i][:, 0:129], T.pts[:, 512 * u + 128 * kp:512 * u + 128 * kp + 128], v_of(s, i),
+                      kp == 0, kp == G - 1).then_inc(S["o_%d" % u], 1)
+
+    pe.wait_ge(S.ld_k, 16)
+    pe.wait_ge(S.ld_qo, 32)
+    pe.wait_ge(S.aq, 2 * len(others))
+    scores(0, True)
+    scores(1, False)
+    pe.wait_ge(S.aqx, len(cable))
+    scores(2, False)
+    scores(3, False)
     pe.wait_ge(S.id, 1)
-    pe.wait_ge(S.ld_v, 16)
-    for b in range(2):
-        for hf in range(2):
-            pe.wait_ge(ev("exp%d" % hf, b), 1)
-            for i in range(4):
-                kp = 4 * hf + i
-                pe.transpose(PT[hf][:, 512 * b + 128 * i:512 * b + 128 * i + 128],
-                             T.p[:, 1024 * b + 128 * kp:1024 * b + 128 * kp + 128], T.ident[:, :]
-                             ).then_inc(ev("t%d" % hf, b), 1)
-        for kp in range(8):
-            if kp % 4 == 0:
-                pe.wait_ge(ev("c%d" % (kp // 4), b), 1)
-            if b == 0 and ko[kp] != r:
-                pe.wait_ge(S["av%d" % ko[kp]], n_in(ko[kp], 1))
-            pe.matmul(OB[b][:, 0:128], T.pts[:, 1024 * b + 128 * kp:1024 * b + 128 * kp + 128], v_of(ko[kp]),
-                      kp == 0, kp == 7).then_inc(ev("o", b), 1)
+    pe.wait_ge(S.onec, 2 * G)
+    pe.wait_ge(S.ld_vo, 16)
+    turn(2)
+    turn(3)
+    pv(2, True)
+    pv(3, False)
+    turn(0)
+    turn(1)
+    pv(0, False)
+    pv(1, False)
 
     v = g.vector
     v.memset(T.zero[:, :], 0.0).then_inc(S.zero, 1)
+    for s in range(G):
+        v.memset(T.vl[:, s, 7:8], 1.0).then_inc(S.onec, 1)
+        v.memset(T.vl[:, s, 264:265], 1.0).then_inc(S.onec, 1)
+    for u in range(4):
+        v.wait_ge(S["s_%d" % u], 4)
+        v.tensor_reduce(shift_col(u), SB[u][:, :], axis=AxisListType.X, op=AluOpType.max, negate=True
+                        ).then_inc(S["nm_%d" % u], 1)
 
-    def take_q(j):
-        if j == r:
-            v.wait_ge(S.ld_qk, 32)
-        else:
-            v.wait_ge(S["aqk%d" % j], n_in(j, 0))
-        c = 128 * blk[j] + QP * slot[j]
-        v.tensor_copy(T.qc[:, c:c + QP], q_of(j)).then_inc(ev("q", blk[j]), 1)
+    def take(u):
+        v.wait_ge(S["t_%d" % u], 4)
+        v.tensor_copy(T.pts[:, 512 * u:512 * u + 512], PT[u % 2][:, 0:512]).then_inc(S["c_%d" % u], 1)
 
-    def neg_max(b, hf):
-        v.wait_ge(ev("s%d" % hf, b), 4)
-        v.tensor_reduce(T.st[:, 8 * b + hf:8 * b + hf + 1], SB[b][:, 512 * hf:512 * hf + 512], axis=AxisListType.X,
-                        op=AluOpType.max, negate=True).then_inc(ev("red", b), 1)
+    take(2)
+    take(3)
+    for i in range(2):
+        v.wait_ge(S["o_%d" % (2 + i)], 4)
+        v.tensor_copy(T.xs[:, POS[i]:POS[i] + 129], OB[i][:, 0:129]).then_inc(S["fx%d" % i], 1)
+    take(0)
+    take(1)
+    v.wait_ge(S.axl, len(eng))
+    v.wait_ge(S.nm_0, 1)
+    v.wait_ge(S.nm_1, 1)
+    v.tensor_tensor(T.dl[:, :], T.xl[:, 258:260], T.nmy[:, :], AluOpType.subtract).then_inc(S.m1, 1)
+    v.wait_ge(S.m1, 1)
+    v.tensor_scalar(T.dd[:, 0:2], T.dl[:, :], 0.0, None, AluOpType.min).then_inc(S.m2, 1)
+    v.tensor_scalar(T.dd[:, 2:4], T.dl[:, :], -1.0, 0.0, AluOpType.mult, AluOpType.min).then_inc(S.m2, 1)
+    v.wait_ge(S.m3, 1)
+    for i in range(2):
+        v.tensor_scalar(T.t2[:, POS[i]:POS[i] + 129], T.xl[:, POS[i]:POS[i] + 129], T.aa[:, 2 + i:3 + i], None,
+                        AluOpType.mult).then_inc(S["m5_%d" % i], 1)
+    for i in range(2):
+        v.wait_ge(S["m4_%d" % i], 1)
+        v.wait_ge(S["m5_%d" % i], 1)
+        v.tensor_tensor(T.sm[:, POS[i]:POS[i] + 129], OB[i][:, 0:129], T.t2[:, POS[i]:POS[i] + 129], AluOpType.add
+                        ).then_inc(S["m6_%d" % i], 1)
+    v.wait_ge(S.m6_0, 1)
+    v.wait_ge(S.m6_1, 1)
+    v.reciprocal(T.rc[:, :], T.sm[:, 128:130]).then_inc(S.m7, 1)
+    v.wait_ge(S.m7, 1)
+    v.tensor_scalar(T.yl[:, 256 * me:256 * me + 128], T.sm[:, OCOL[0]:OCOL[0] + 128], T.rc[:, 1:2], None,
+                    AluOpType.mult).then_inc(S.fy0, 1)
 
-    def join_max(b):
-        v.wait_ge(ev("red", b), 2)
-        v.tensor_tensor(T.st[:, 8 * b + 2:8 * b + 3], T.st[:, 8 * b:8 * b + 1], T.st[:, 8 * b + 1:8 * b + 2],
-                        AluOpType.min).then_inc(ev("nm", b), 1)
-
-    for j in [r] + ys + xnear:
-        take_q(j)
-    neg_max(1, 0)
-    for j in far[r]:
-        take_q(j)
-    neg_max(0, 0)
-    neg_max(0, 1)
-    join_max(0)
-    neg_max(1, 1)
-    join_max(1)
-    for b in range(2):
-        for hf in range(2):
-            v.wait_ge(ev("t%d" % hf, b), 4)
-            v.tensor_copy(T.pts[:, 1024 * b + 512 * hf:1024 * b + 512 * hf + 512],
-                          PT[hf][:, 512 * b:512 * b + 512]).then_inc(ev("c%d" % hf, b), 1)
-            if hf == 0:
-                v.wait_ge(ev("exp0", b), 1)
-                v.wait_ge(ev("exp1", b), 1)
-                v.tensor_tensor(T.st[:, 8 * b + 5:8 * b + 6], T.st[:, 8 * b + 3:8 * b + 4], T.st[:, 8 * b + 4:8 * b + 5],
-                                AluOpType.add).then_inc(ev("l", b), 1)
-                v.wait_ge(ev("l", b), 1)
-                v.reciprocal(T.st[:, 8 * b + 6:8 * b + 7], T.st[:, 8 * b + 5:8 * b + 6]).then_inc(ev("rl", b), 1)
-        v.wait_ge(ev("o", b), 8)
-        v.wait_ge(ev("rl", b), 1)
-        v.tensor_scalar(T.yqx[:, :] if b == 0 else vcol(T.yl, r), OB[b][:, 0:128], T.st[:, 8 * b + 6:8 * b + 7], None,
-                        AluOpType.mult).then_inc(ev("f", b), 1)
-
-    for w in R:
-        if w != r:
-            g.sync.wait_ge(S["ay%d" % w], half if r in far[w] else len(eng))
-    g.sync.wait_ge(ev("f", 1), 1)
-    g.sync.dma_start(T.y[:, :], T.yl[QP * slot[r]:QP * slot[r] + QP, :]).then_inc(S.st_y, 16)
+    for j in others:
+        g.sync.wait_ge(S["ay%d" % idx[j]], len(eng))
+    g.sync.wait_ge(S.fy0, 1)
+    g.sync.wait_ge(S.fy1, 1)
+    g.sync.dma_start(T.y[:, :], T.yl[QP * me:QP * me + QP, :]).then_inc(S.st_y, 16)
     g.sync.wait_ge(S.st_y, 16)

@@ -3,10 +3,6 @@ from concourse.mybir import AluOpType, AxisListType, ActivationFunctionType
 
 N, NH, QP, KP = 8, 8, 32, 128
 G = 4
-VW = 272
-PW = 2 * 129 + 2
-POS = [129, 0]
-OCOL = [130, 0]
 
 SCRATCH = {
     "qs": ("sbuf", [128, NH * QP], "bfloat16"),
@@ -14,21 +10,24 @@ SCRATCH = {
     "vs": ("sbuf", [128, NH * 128], "bfloat16"),
     "ql": ("sbuf", [128, 512], "bfloat16"),
     "kl": ("sbuf", [128, G, 256], "bfloat16"),
-    "vl": ("sbuf", [128, G, VW], "bfloat16"),
+    "vl": ("sbuf", [128, G, 256], "bfloat16"),
     "zero": ("sbuf", [128, 128], "bfloat16"),
     "ones": ("sbuf", [128, 128], "bfloat16"),
     "ident": ("sbuf", [128, 128], "bfloat16"),
     "p": ("sbuf", [128, 2048], "bfloat16"),
     "pts": ("sbuf", [128, 2048], "bfloat16"),
-    "nmy": ("sbuf", [128, 2], "bfloat16"),
-    "xs": ("sbuf", [128, PW], "bfloat16"),
-    "xl": ("sbuf", [128, PW], "bfloat16"),
+    "st": ("sbuf", [128, 8], "float32"),
+    "sl": ("sbuf", [128, 4], "float32"),
+    "xs": ("sbuf", [128, 256], "bfloat16"),
+    "xl": ("sbuf", [128, 256], "bfloat16"),
     "dl": ("sbuf", [128, 2], "float32"),
     "dd": ("sbuf", [128, 4], "float32"),
     "aa": ("sbuf", [128, 4], "float32"),
-    "t2": ("sbuf", [128, 258], "float32"),
-    "sm": ("sbuf", [128, 258], "float32"),
+    "al": ("sbuf", [128, 4], "float32"),
+    "den": ("sbuf", [128, 2], "float32"),
     "rc": ("sbuf", [128, 2], "float32"),
+    "cc": ("sbuf", [128, 4], "float32"),
+    "t2": ("sbuf", [128, 256], "float32"),
     "yl": ("sbuf", [128, NH * 128], "bfloat16"),
     "s0": ("psum", [128, 512], "float32"),
     "s1": ("psum", [128, 512], "float32"),
@@ -40,11 +39,11 @@ SCRATCH = {
     "ob": ("psum", [128, 512], "float32"),
 }
 
-SEMAPHORES = (["ld_q", "ld_k", "ld_v", "ld_qo", "ld_vo", "st_y", "snd", "zero", "ones", "id", "onec",
-               "aq", "aqx", "axl", "m1", "m2", "m3", "m7"]
+SEMAPHORES = (["ld_q", "ld_k", "ld_v", "st_y", "snd", "zero", "ones", "id", "cq",
+               "aq", "aqx", "asl", "axl", "m1", "m2", "m3", "m4", "m5", "m6", "m7"]
               + ["ak%d" % s for s in range(G)] + ["av%d" % s for s in range(G)] + ["ay%d" % s for s in range(G)]
               + ["%s%d" % (e, u) for e in ("s_", "nm_", "e_", "t_", "c_", "o_") for u in range(4)]
-              + ["%s%d" % (e, i) for e in ("fx", "fy", "m4_", "m5_", "m6_") for i in range(2)])
+              + ["%s%d" % (e, i) for e in ("fx", "fy", "ow", "tt") for i in range(2)])
 
 
 def _bits(m):
@@ -106,18 +105,22 @@ def rank_program(g, core, T, topo):
         return T.ks[:, 256 * me + 128 * i:256 * me + 128 * i + 128] if s == me else T.kl[:, s, 128 * i:128 * i + 128]
 
     def v_of(s, i):
-        return T.vl[:, s, 7:136] if i == 0 else T.vl[:, s, 136:265]
+        return T.vs[:, 256 * me + 128 * i:256 * me + 128 * i + 128] if s == me else T.vl[:, s, 128 * i:128 * i + 128]
+
+    def shift_col(u):
+        c = 4 * (u // 2) + u % 2
+        return T.st[:, c:c + 1]
+
+    def l_col(u):
+        c = 4 * (u // 2) + 2 + u % 2
+        return T.st[:, c:c + 1]
 
     ko = [me] + [idx[j] for j in others]
     SB, PT, OB = [T.s0, T.s1, T.s2, T.s3], [T.pta, T.ptb], [T.oa, T.ob]
 
     g.scalar.dma_start(T.qs[:, :], T.q[:, :]).then_inc(S.ld_q, 16)
     g.sync.dma_start(T.ks[:, :], T.k[:, :]).then_inc(S.ld_k, 16)
-    for i in range(2):
-        h = 2 * me + i
-        g.scalar.dma_start(T.ql[:, 128 * i + QP * me:128 * i + QP * me + QP], T.q[:, QP * h:QP * h + QP]).then_inc(S.ld_qo, 16)
     g.sync.dma_start(T.vs[:, :], T.v[:, :]).then_inc(S.ld_v, 16)
-    g.scalar.dma_start(T.vl[:, me, 8:264], T.v[:, 256 * me:256 * me + 256]).then_inc(S.ld_vo, 16)
 
     g.wait_ge(S.ld_q, 16)
     call = []
@@ -133,13 +136,16 @@ def rank_program(g, core, T, topo):
     g.remote_dma_fused([tr(T.ks[:, 256 * idx[d]:256 * idx[d] + 256], T.kl[:, me, :], [d], S["ak%d" % me], lane[t])
                         for t, d in enumerate(others)], local_sem=S.snd)
     g.wait_ge(S.ld_v, 16)
-    g.remote_dma_fused([tr(T.vs[:, 256 * idx[d]:256 * idx[d] + 256], T.vl[:, me, 8:264], [d], S["av%d" % me], lane[t])
+    g.remote_dma_fused([tr(T.vs[:, 256 * idx[d]:256 * idx[d] + 256], T.vl[:, me, :], [d], S["av%d" % me], lane[t])
                         for t, d in enumerate(others)], local_sem=S.snd)
-    g.wait_ge(S.ld_qo, 32)
+    g.wait_ge(S.cq, 2)
     g.wait_ge(S.aq, 2 * len(others))
     g.remote_dma_fused([tr(T.ql[:, 0:256], T.ql[:, 256:512], [mate], S.aqx, cable)], local_sem=S.snd)
+    for u in (2, 3):
+        g.wait_ge(S["nm_%d" % u], 1)
+        g.wait_ge(S["e_%d" % u], 1)
+    g.remote_dma_fused([tr(T.st[:, 4:8], T.sl[:, :], [mate], S.asl, eng)], local_sem=S.snd)
     for i in range(2):
-        g.wait_ge(S["nm_%d" % (2 + i)], 1)
         g.wait_ge(S["fx%d" % i], 1)
     g.remote_dma_fused([tr(T.xs[:, :], T.xl[:, :], [mate], S.axl, eng)], local_sem=S.snd)
     for i in range(2):
@@ -151,22 +157,20 @@ def rank_program(g, core, T, topo):
     a = g.scalar
     a.wait_ge(S.zero, 1)
     a.activation(T.ones[:, :], T.zero[:, :], EXP).then_inc(S.ones, 1)
-
-    def shift_col(u):
-        return T.nmy[:, u:u + 1] if u < 2 else T.xs[:, 258 + u - 2:258 + u - 1]
-
     for u in range(4):
         a.wait_ge(S["nm_%d" % u], 1)
-        a.activation(T.p[:, 512 * u:512 * u + 512], SB[u][:, :], EXP, bias=shift_col(u), scale=1.0).then_inc(S["e_%d" % u], 1)
+        a.activation(T.p[:, 512 * u:512 * u + 512], SB[u][:, :], EXP, bias=shift_col(u), scale=1.0,
+                     accum_out=l_col(u)).then_inc(S["e_%d" % u], 1)
+    a.wait_ge(S.o_3, 4)
+    a.activation(T.xs[:, 128:256], OB[1][:, 0:128], CPY).then_inc(S.fx1, 1)
     a.wait_ge(S.m2, 2)
     a.activation(T.aa[:, :], T.dd[:, :], EXP).then_inc(S.m3, 1)
-    a.wait_ge(S.m3, 1)
+    a.wait_ge(S.m7, 2)
     for i in range(2):
         a.wait_ge(S["o_%d" % i], 4)
-        a.activation(OB[i][:, 0:129], OB[i][:, 0:129], CPY, scale=T.aa[:, i:i + 1]).then_inc(S["m4_%d" % i], 1)
-    a.wait_ge(S.m7, 1)
-    a.activation(T.yl[:, 256 * me + 128:256 * me + 256], T.sm[:, OCOL[1]:OCOL[1] + 128], CPY,
-                 scale=T.rc[:, 0:1]).then_inc(S.fy1, 1)
+        a.activation(OB[i][:, 0:128], OB[i][:, 0:128], CPY, scale=T.cc[:, i:i + 1]).then_inc(S["ow%d" % i], 1)
+    a.wait_ge(S.axl, len(eng))
+    a.activation(T.t2[:, 128:256], T.xl[:, 128:256], CPY, scale=T.cc[:, 3:4]).then_inc(S.tt1, 1)
 
     pe = g.tensor
 
@@ -184,19 +188,12 @@ def rank_program(g, core, T, topo):
             pe.transpose(PT[u % 2][:, 128 * kp:128 * kp + 128], T.p[:, 512 * u + 128 * kp:512 * u + 128 * kp + 128],
                          T.ident[:, :]).then_inc(S["t_%d" % u], 1)
 
-    def pv(u, first):
-        i = u % 2
-        pe.wait_ge(S["c_%d" % u], 1)
-        if u < 2:
-            pe.wait_ge(S["fx%d" % i], 1)
-        for kp, s in enumerate(ko):
-            if first and s != me:
-                pe.wait_ge(S["av%d" % s], per)
-            pe.matmul(OB[i][:, 0:129], T.pts[:, 512 * u + 128 * kp:512 * u + 128 * kp + 128], v_of(s, i),
-                      kp == 0, kp == G - 1).then_inc(S["o_%d" % u], 1)
+    def pv1(u, kp, s):
+        pe.matmul(OB[u % 2][:, 0:128], T.pts[:, 512 * u + 128 * kp:512 * u + 128 * kp + 128], v_of(s, u % 2),
+                  kp == 0, kp == G - 1).then_inc(S["o_%d" % u], 1)
 
     pe.wait_ge(S.ld_k, 16)
-    pe.wait_ge(S.ld_qo, 32)
+    pe.wait_ge(S.cq, 2)
     pe.wait_ge(S.aq, 2 * len(others))
     scores(0, True)
     scores(1, False)
@@ -204,22 +201,30 @@ def rank_program(g, core, T, topo):
     scores(2, False)
     scores(3, False)
     pe.wait_ge(S.id, 1)
-    pe.wait_ge(S.onec, 2 * G)
-    pe.wait_ge(S.ld_vo, 16)
     turn(2)
     turn(3)
-    pv(2, True)
-    pv(3, False)
+    pe.wait_ge(S.ld_v, 16)
+    for kp, s in enumerate(ko):
+        if s != me:
+            pe.wait_ge(S["av%d" % s], per)
+        for u in (2, 3):
+            if kp == 0:
+                pe.wait_ge(S["c_%d" % u], 1)
+            pv1(u, kp, s)
     turn(0)
     turn(1)
-    pv(0, False)
-    pv(1, False)
+    for u in (0, 1):
+        pe.wait_ge(S["c_%d" % u], 1)
+        pe.wait_ge(S["fx%d" % u], 1)
+        for kp, s in enumerate(ko):
+            pv1(u, kp, s)
 
     v = g.vector
     v.memset(T.zero[:, :], 0.0).then_inc(S.zero, 1)
-    for s in range(G):
-        v.memset(T.vl[:, s, 7:8], 1.0).then_inc(S.onec, 1)
-        v.memset(T.vl[:, s, 264:265], 1.0).then_inc(S.onec, 1)
+    v.wait_ge(S.ld_q, 16)
+    for i in range(2):
+        h = 2 * me + i
+        v.tensor_copy(T.ql[:, 128 * i + QP * me:128 * i + QP * me + QP], T.qs[:, QP * h:QP * h + QP]).then_inc(S.cq, 1)
     for u in range(4):
         v.wait_ge(S["s_%d" % u], 4)
         v.tensor_reduce(shift_col(u), SB[u][:, :], axis=AxisListType.X, op=AluOpType.max, negate=True
@@ -231,33 +236,37 @@ def rank_program(g, core, T, topo):
 
     take(2)
     take(3)
-    for i in range(2):
-        v.wait_ge(S["o_%d" % (2 + i)], 4)
-        v.tensor_copy(T.xs[:, POS[i]:POS[i] + 129], OB[i][:, 0:129]).then_inc(S["fx%d" % i], 1)
+    v.wait_ge(S.o_2, 4)
+    v.tensor_copy(T.xs[:, 0:128], OB[0][:, 0:128]).then_inc(S.fx0, 1)
     take(0)
     take(1)
-    v.wait_ge(S.axl, len(eng))
+    v.wait_ge(S.asl, len(eng))
     v.wait_ge(S.nm_0, 1)
     v.wait_ge(S.nm_1, 1)
-    v.tensor_tensor(T.dl[:, :], T.xl[:, 258:260], T.nmy[:, :], AluOpType.subtract).then_inc(S.m1, 1)
+    v.tensor_tensor(T.dl[:, :], T.sl[:, 0:2], T.st[:, 0:2], AluOpType.subtract).then_inc(S.m1, 1)
     v.wait_ge(S.m1, 1)
     v.tensor_scalar(T.dd[:, 0:2], T.dl[:, :], 0.0, None, AluOpType.min).then_inc(S.m2, 1)
     v.tensor_scalar(T.dd[:, 2:4], T.dl[:, :], -1.0, 0.0, AluOpType.mult, AluOpType.min).then_inc(S.m2, 1)
     v.wait_ge(S.m3, 1)
+    v.wait_ge(S.e_0, 1)
+    v.wait_ge(S.e_1, 1)
+    v.tensor_tensor(T.al[:, 0:2], T.aa[:, 0:2], T.st[:, 2:4], AluOpType.mult).then_inc(S.m4, 1)
+    v.tensor_tensor(T.al[:, 2:4], T.aa[:, 2:4], T.sl[:, 2:4], AluOpType.mult).then_inc(S.m4, 1)
+    v.wait_ge(S.m4, 2)
+    v.tensor_tensor(T.den[:, :], T.al[:, 0:2], T.al[:, 2:4], AluOpType.add).then_inc(S.m5, 1)
+    v.wait_ge(S.m5, 1)
+    v.reciprocal(T.rc[:, :], T.den[:, :]).then_inc(S.m6, 1)
+    v.wait_ge(S.m6, 1)
+    v.tensor_tensor(T.cc[:, 0:2], T.aa[:, 0:2], T.rc[:, :], AluOpType.mult).then_inc(S.m7, 1)
+    v.tensor_tensor(T.cc[:, 2:4], T.aa[:, 2:4], T.rc[:, :], AluOpType.mult).then_inc(S.m7, 1)
+    v.wait_ge(S.m7, 2)
+    v.wait_ge(S.axl, len(eng))
+    v.tensor_scalar(T.t2[:, 0:128], T.xl[:, 0:128], T.cc[:, 2:3], None, AluOpType.mult).then_inc(S.tt0, 1)
     for i in range(2):
-        v.tensor_scalar(T.t2[:, POS[i]:POS[i] + 129], T.xl[:, POS[i]:POS[i] + 129], T.aa[:, 2 + i:3 + i], None,
-                        AluOpType.mult).then_inc(S["m5_%d" % i], 1)
-    for i in range(2):
-        v.wait_ge(S["m4_%d" % i], 1)
-        v.wait_ge(S["m5_%d" % i], 1)
-        v.tensor_tensor(T.sm[:, POS[i]:POS[i] + 129], OB[i][:, 0:129], T.t2[:, POS[i]:POS[i] + 129], AluOpType.add
-                        ).then_inc(S["m6_%d" % i], 1)
-    v.wait_ge(S.m6_0, 1)
-    v.wait_ge(S.m6_1, 1)
-    v.reciprocal(T.rc[:, :], T.sm[:, 128:130]).then_inc(S.m7, 1)
-    v.wait_ge(S.m7, 1)
-    v.tensor_scalar(T.yl[:, 256 * me:256 * me + 128], T.sm[:, OCOL[0]:OCOL[0] + 128], T.rc[:, 1:2], None,
-                    AluOpType.mult).then_inc(S.fy0, 1)
+        v.wait_ge(S["tt%d" % i], 1)
+        v.wait_ge(S["ow%d" % i], 1)
+        v.tensor_tensor(T.yl[:, 256 * me + 128 * i:256 * me + 128 * i + 128], OB[i][:, 0:128],
+                        T.t2[:, 128 * i:128 * i + 128], AluOpType.add).then_inc(S["fy%d" % i], 1)
 
     for j in others:
         g.sync.wait_ge(S["ay%d" % idx[j]], len(eng))

@@ -3,47 +3,51 @@ from concourse.mybir import AluOpType, AxisListType, ActivationFunctionType
 
 N, NH, QP, KP = 8, 8, 32, 128
 G = 4
+HW = 4
 
 SCRATCH = {
     "qs": ("sbuf", [128, NH * QP], "bfloat16"),
     "ks": ("sbuf", [128, NH * KP], "bfloat16"),
     "vs": ("sbuf", [128, NH * 128], "bfloat16"),
-    "ql": ("sbuf", [128, 512], "bfloat16"),
-    "kl": ("sbuf", [128, G, 256], "bfloat16"),
-    "vl": ("sbuf", [128, G, 256], "bfloat16"),
+    "qin": ("sbuf", [128, G, HW * QP], "bfloat16"),
+    "ql": ("sbuf", [128, HW * 128], "bfloat16"),
+    "kl": ("sbuf", [128, G, HW * KP], "bfloat16"),
+    "vl": ("sbuf", [128, G, HW * 128], "bfloat16"),
     "zero": ("sbuf", [128, 128], "bfloat16"),
     "ones": ("sbuf", [128, 128], "bfloat16"),
     "ident": ("sbuf", [128, 128], "bfloat16"),
     "p": ("sbuf", [128, 2048], "bfloat16"),
     "pts": ("sbuf", [128, 2048], "bfloat16"),
     "st": ("sbuf", [128, 8], "float32"),
-    "sl": ("sbuf", [128, 4], "float32"),
-    "xs": ("sbuf", [128, 256], "bfloat16"),
-    "xl": ("sbuf", [128, 256], "bfloat16"),
-    "dl": ("sbuf", [128, 2], "float32"),
-    "dd": ("sbuf", [128, 4], "float32"),
-    "aa": ("sbuf", [128, 4], "float32"),
-    "al": ("sbuf", [128, 4], "float32"),
-    "den": ("sbuf", [128, 2], "float32"),
-    "rc": ("sbuf", [128, 2], "float32"),
-    "cc": ("sbuf", [128, 4], "float32"),
-    "t2": ("sbuf", [128, 256], "float32"),
-    "yl": ("sbuf", [128, NH * 128], "bfloat16"),
+    "sl": ("sbuf", [128, 32], "float32"),
+    "xs": ("sbuf", [128, G, 128], "bfloat16"),
+    "xl": ("sbuf", [128, G, 128], "bfloat16"),
+    "dl": ("sbuf", [128, 16], "float32"),
+    "dd": ("sbuf", [128, 32], "float32"),
+    "aa": ("sbuf", [128, 32], "float32"),
+    "al": ("sbuf", [128, 28], "float32"),
+    "den": ("sbuf", [128, 12], "float32"),
+    "dm": ("sbuf", [128, 12], "float32"),
+    "rc": ("sbuf", [128, 12], "float32"),
+    "cc": ("sbuf", [128, 32], "float32"),
+    "ee": ("sbuf", [128, 512], "bfloat16"),
+    "zz": ("sbuf", [128, 512], "bfloat16"),
+    "yl": ("sbuf", [128, 256], "bfloat16"),
     "s0": ("psum", [128, 512], "float32"),
     "s1": ("psum", [128, 512], "float32"),
     "s2": ("psum", [128, 512], "float32"),
     "s3": ("psum", [128, 512], "float32"),
     "pta": ("psum", [128, 1024], "bfloat16"),
     "ptb": ("psum", [128, 1024], "bfloat16"),
-    "oa": ("psum", [128, 512], "float32"),
-    "ob": ("psum", [128, 512], "float32"),
+    "cb": ("psum", [128, 512], "float32"),
+    "ya": ("psum", [128, 512], "float32"),
 }
 
-SEMAPHORES = (["ld_q", "ld_k", "ld_v", "st_y", "snd", "zero", "ones", "id", "cq",
-               "aq", "aqx", "asl", "axl", "m1", "m2", "m3", "m4", "m5", "m6", "m7"]
-              + ["ak%d" % s for s in range(G)] + ["av%d" % s for s in range(G)] + ["ay%d" % s for s in range(G)]
-              + ["%s%d" % (e, u) for e in ("s_", "nm_", "e_", "t_", "c_", "o_") for u in range(4)]
-              + ["%s%d" % (e, i) for e in ("fx", "fy", "ow", "tt") for i in range(2)])
+SEMAPHORES = (["ld_q", "ld_k", "ld_v", "snd", "zero", "ones", "id", "aq", "asl", "cbm",
+               "m1", "m2", "m3", "m4", "m5", "m6", "m7", "m8"]
+              + ["%s%d_%d" % (e, s, hp) for e in ("ak", "av") for s in range(G) for hp in range(2)]
+              + ["%s%d" % (e, u) for e in ("cq", "s_", "nm_", "e_", "t_", "c_", "o_", "fx", "ax", "ee", "z") for u in range(4)]
+              + ["%s%d" % (e, i) for e in ("yy", "fy", "st_y") for i in range(2)])
 
 
 def _bits(m):
@@ -60,13 +64,16 @@ def _mk(bs):
 def _plan(T, topo):
     C = [int(c) for c in T.cores]
     R = range(len(C))
-    rack = [topo.rack(topo.host(c)) for c in C]
+    host = [topo.host(c) for c in C]
+    rack = [topo.rack(h) for h in host]
     chip = [topo.chip(c) for c in C]
-    partner = [[j for j in R if rack[j] != rack[r] and chip[j] == chip[r] and topo.may_write(C[r], C[j])][0] for r in R]
-    base = [j for j in R if rack[j] == rack[0]]
-    idx = [base.index(j) if j in base else base.index(partner[j]) for j in R]
+    chips, racks = sorted(set(chip)), sorted(set(rack))
+    half = [chips.index(x) for x in chip]
+    slot = [racks.index(rack[j]) * len(chips) + half[j] for j in R]
+    near = [[j for j in R if host[j] != host[r] and topo.may_write(C[r], C[j]) and topo.may_write(C[j], C[r])] for r in R]
     grp = [[j for j in R if rack[j] == rack[r]] for r in R]
-    return dict(C=C, partner=partner, idx=idx, grp=grp)
+    kslot = [grp[j].index(j) for j in R]
+    return dict(C=C, rack=rack, half=half, slot=slot, near=near, grp=grp, kslot=kslot)
 
 
 def rank_program(g, core, T, topo):
@@ -74,203 +81,223 @@ def rank_program(g, core, T, topo):
     if r is None:
         return
     P = _plan(T, topo)
-    C, idx = P["C"], P["idx"]
-    me = idx[r]
-    mate = P["partner"][r]
-    others = [j for j in P["grp"][r] if j != r]
+    C, rack, half, slot, kslot = P["C"], P["rack"], P["half"], P["slot"], P["kslot"]
+    me = kslot[r]
+    near = P["near"][r]
+    others = sorted([j for j in P["grp"][r] if j != r], key=lambda d: (kslot[d] - me) % G)
     S = T.sem
     EXP = ActivationFunctionType.Exp
     CPY = ActivationFunctionType.Copy
 
     m = 0xFFFF
-    for j in others + [mate]:
+    for j in others + near:
         m &= topo.mask(core, C[j])
     eng = _bits(m)
-    per = len(eng) // (len(others) + 1)
-    lane = [eng[per * t:per * t + per] for t in range(len(others) + 1)]
-    cable = lane[len(others)]
+    per = len(eng) // 4
+    lane = [eng[per * t:per * t + per] for t in range(4)]
 
     sent = [0]
 
-    def tr(src, dst, dsts, sem, engs):
-        ids = []
-        for d in dsts:
-            rid, pid = topo.addr(C[d], core)
-            ids.append(DstId(rid=rid, pnc=pid))
+    def tr(src, dst, d, sem, engs):
+        rid, pid = topo.addr(C[d], core)
         sent[0] += len(engs)
-        return RemoteDMATransfer(dst_ids=ids, dma_engine_mask=_mk(engs), remote_sem=sem, srcs=[src],
-                                 dsts=[dst for _ in dsts], alu_op=0)
+        return RemoteDMATransfer(dst_ids=[DstId(rid=rid, pnc=pid)], dma_engine_mask=_mk(engs), remote_sem=sem, srcs=[src],
+                                 dsts=[dst], alu_op=0)
+
+    def piece(w, o):
+        return (0 if rack[w] == rack[o] else 1) * 2 + half[w]
 
     def k_of(s, i):
-        return T.ks[:, 256 * me + 128 * i:256 * me + 128 * i + 128] if s == me else T.kl[:, s, 128 * i:128 * i + 128]
+        c = 512 * half[r] + 128 * i
+        return T.ks[:, c:c + 128] if s == me else T.kl[:, s, 128 * i:128 * i + 128]
 
     def v_of(s, i):
-        return T.vs[:, 256 * me + 128 * i:256 * me + 128 * i + 128] if s == me else T.vl[:, s, 128 * i:128 * i + 128]
+        c = 512 * half[r] + 128 * i
+        return T.vs[:, c:c + 128] if s == me else T.vl[:, s, 128 * i:128 * i + 128]
 
-    def shift_col(u):
-        c = 4 * (u // 2) + u % 2
-        return T.st[:, c:c + 1]
-
-    def l_col(u):
-        c = 4 * (u // 2) + 2 + u % 2
-        return T.st[:, c:c + 1]
-
-    ko = [me] + [idx[j] for j in others]
-    SB, PT, OB = [T.s0, T.s1, T.s2, T.s3], [T.pta, T.ptb], [T.oa, T.ob]
+    ko = [me] + sorted([s for s in range(G) if s != me], key=lambda s: (me - s) % G)
+    SB, PT = [T.s0, T.s1, T.s2, T.s3], [T.pta, T.ptb]
+    Y = [T.ya, T.s0]
 
     g.scalar.dma_start(T.qs[:, :], T.q[:, :]).then_inc(S.ld_q, 16)
     g.sync.dma_start(T.ks[:, :], T.k[:, :]).then_inc(S.ld_k, 16)
     g.sync.dma_start(T.vs[:, :], T.v[:, :]).then_inc(S.ld_v, 16)
 
     g.wait_ge(S.ld_q, 16)
-    call = []
-    for t, d in enumerate(others):
-        for i in range(2):
-            h = 2 * idx[d] + i
-            call.append(tr(T.qs[:, QP * h:QP * h + QP], T.ql[:, 128 * i + QP * me:128 * i + QP * me + QP], [d], S.aq,
-                           [lane[t][i]]))
-    g.remote_dma_fused(call, local_sem=S.snd)
+    g.remote_dma_fused([tr(T.qs[:, 128 * half[w]:128 * half[w] + 128], T.qin[:, slot[r], :], w, S.aq, lane[t])
+                        for t, w in enumerate(near)], local_sem=S.snd)
     g.wait_ge(S.ones, 1)
     g.affine_select(T.ident[:, :], T.ones[:, :], [[-1, 128]], AluOpType.is_equal, 0.0, 0, 1).then_inc(S.id, 1)
+    seq = [(kind, hp, d) for kind in "kv" for hp in range(2) for d in others]
     g.wait_ge(S.ld_k, 16)
-    g.remote_dma_fused([tr(T.ks[:, 256 * idx[d]:256 * idx[d] + 256], T.kl[:, me, :], [d], S["ak%d" % me], lane[t])
-                        for t, d in enumerate(others)], local_sem=S.snd)
-    g.wait_ge(S.ld_v, 16)
-    g.remote_dma_fused([tr(T.vs[:, 256 * idx[d]:256 * idx[d] + 256], T.vl[:, me, :], [d], S["av%d" % me], lane[t])
-                        for t, d in enumerate(others)], local_sem=S.snd)
-    g.wait_ge(S.cq, 2)
-    g.wait_ge(S.aq, 2 * len(others))
-    g.remote_dma_fused([tr(T.ql[:, 0:256], T.ql[:, 256:512], [mate], S.aqx, cable)], local_sem=S.snd)
-    for u in (2, 3):
+    have_v = False
+    for c0 in range(0, len(seq), 4):
+        chunk = seq[c0:c0 + 4]
+        if not have_v and any(kind == "v" for kind, hp, d in chunk):
+            g.wait_ge(S.ld_v, 16)
+            have_v = True
+        call = []
+        for t, (kind, hp, d) in enumerate(chunk):
+            c = 512 * half[d] + 256 * hp
+            src = T.ks[:, c:c + 256] if kind == "k" else T.vs[:, c:c + 256]
+            dst = (T.kl if kind == "k" else T.vl)[:, me, 256 * hp:256 * hp + 256]
+            call.append(tr(src, dst, d, S["a%s%d_%d" % (kind, me, hp)], lane[t]))
+        g.remote_dma_fused(call, local_sem=S.snd)
+    for u in range(4):
         g.wait_ge(S["nm_%d" % u], 1)
         g.wait_ge(S["e_%d" % u], 1)
-    g.remote_dma_fused([tr(T.st[:, 4:8], T.sl[:, :], [mate], S.asl, eng)], local_sem=S.snd)
-    for i in range(2):
-        g.wait_ge(S["fx%d" % i], 1)
-    g.remote_dma_fused([tr(T.xs[:, :], T.xl[:, :], [mate], S.axl, eng)], local_sem=S.snd)
-    for i in range(2):
-        g.wait_ge(S["fy%d" % i], 1)
-    g.remote_dma_fused([tr(T.yl[:, 256 * me:256 * me + 256], T.yl[:, 256 * me:256 * me + 256], others, S["ay%d" % me], eng)],
-                       local_sem=S.snd)
+    g.remote_dma_fused([tr(T.st[:, :], T.sl[:, 8 * piece(r, o):8 * piece(r, o) + 8], o, S.asl, lane[t])
+                        for t, o in enumerate(near)], local_sem=S.snd)
+    for u in range(4):
+        g.wait_ge(S["fx%d" % u], 4)
+    g.remote_dma_fused([tr(T.xs[:, slot[o], :], T.xl[:, piece(r, o), :], o, S["ax%d" % piece(r, o)], lane[t])
+                        for t, o in enumerate(near)], local_sem=S.snd)
     g.wait_ge(S.snd, sent[0])
+
+    isel = T.ident[:, QP * slot[r]:QP * slot[r] + QP]
+
+    def e_out(w, i):
+        return T.ee[:, 128 * w + i:128 * w + 128:4]
 
     a = g.scalar
     a.wait_ge(S.zero, 1)
     a.activation(T.ones[:, :], T.zero[:, :], EXP).then_inc(S.ones, 1)
+    a.wait_ge(S.aq, 4 * per)
+    for i in (2, 3):
+        for s in range(G):
+            a.activation(T.ql[:, 128 * i + QP * s:128 * i + QP * s + QP], T.qin[:, s, QP * i:QP * i + QP], CPY
+                         ).then_inc(S["cq%d" % i], 1)
     for u in range(4):
         a.wait_ge(S["nm_%d" % u], 1)
-        a.activation(T.p[:, 512 * u:512 * u + 512], SB[u][:, :], EXP, bias=shift_col(u), scale=1.0,
-                     accum_out=l_col(u)).then_inc(S["e_%d" % u], 1)
-    a.wait_ge(S.o_3, 4)
-    a.activation(T.xs[:, 128:256], OB[1][:, 0:128], CPY).then_inc(S.fx1, 1)
+        a.activation(T.p[:, 512 * u:512 * u + 512], SB[u][:, :], EXP, bias=T.st[:, u:u + 1], scale=1.0,
+                     accum_out=T.st[:, 4 + u:5 + u]).then_inc(S["e_%d" % u], 1)
+    for u in (1, 3):
+        a.wait_ge(S["o_%d" % u], 4)
+        for s in range(G):
+            a.activation(T.xs[:, s, u:128:4], SB[u][:, QP * s:QP * s + QP], CPY).then_inc(S["fx%d" % u], 1)
     a.wait_ge(S.m2, 2)
     a.activation(T.aa[:, :], T.dd[:, :], EXP).then_inc(S.m3, 1)
-    a.wait_ge(S.m7, 2)
-    for i in range(2):
-        a.wait_ge(S["o_%d" % i], 4)
-        a.activation(OB[i][:, 0:128], OB[i][:, 0:128], CPY, scale=T.cc[:, i:i + 1]).then_inc(S["ow%d" % i], 1)
-    a.wait_ge(S.axl, len(eng))
-    a.activation(T.t2[:, 128:256], T.xl[:, 128:256], CPY, scale=T.cc[:, 3:4]).then_inc(S.tt1, 1)
+    a.wait_ge(S.m8, 2)
+    a.wait_ge(S.id, 1)
+    for w in (2, 3):
+        for i in range(HW):
+            a.activation(e_out(w, i), isel, CPY, scale=T.cc[:, 8 * w + i:8 * w + i + 1]).then_inc(S["ee%d" % w], 1)
+    a.wait_ge(S.yy1, 2)
+    a.activation(T.yl[:, 128:256], Y[1][:, 0:128], CPY).then_inc(S.fy1, 1)
+    a.wait_ge(S.fy1, 1)
+    a.dma_start(T.y[:, 512:1024], T.yl[:, 128:256]).then_inc(S.st_y1, 16)
+    a.wait_ge(S.st_y1, 16)
 
     pe = g.tensor
 
-    def scores(u, first):
-        b, i = u // 2, u % 2
+    def scores(u):
+        pe.wait_ge(S["cq%d" % u], 4)
         for kp, s in enumerate(ko):
-            if first and s != me:
-                pe.wait_ge(S["ak%d" % s], per)
-            pe.matmul(SB[u][:, 128 * kp:128 * kp + 128], T.ql[:, 256 * b + 128 * i:256 * b + 128 * i + 128], k_of(s, i),
+            if u % 2 == 0 and s != me:
+                pe.wait_ge(S["ak%d_%d" % (s, u // 2)], per)
+            pe.matmul(SB[u][:, 128 * kp:128 * kp + 128], T.ql[:, 128 * u:128 * u + 128], k_of(s, u),
                       True, True).then_inc(S["s_%d" % u], 1)
 
     def turn(u):
         pe.wait_ge(S["e_%d" % u], 1)
+        if u >= 2:
+            pe.wait_ge(S["c_%d" % (u - 2)], 1)
         for kp in range(G):
             pe.transpose(PT[u % 2][:, 128 * kp:128 * kp + 128], T.p[:, 512 * u + 128 * kp:512 * u + 128 * kp + 128],
                          T.ident[:, :]).then_inc(S["t_%d" % u], 1)
 
-    def pv1(u, kp, s):
-        pe.matmul(OB[u % 2][:, 0:128], T.pts[:, 512 * u + 128 * kp:512 * u + 128 * kp + 128], v_of(s, u % 2),
-                  kp == 0, kp == G - 1).then_inc(S["o_%d" % u], 1)
+    def pv(us, first):
+        for u in us:
+            pe.wait_ge(S["c_%d" % u], 1)
+        for kp, s in enumerate(ko):
+            if first and s != me:
+                pe.wait_ge(S["av%d_%d" % (s, us[0] // 2)], per)
+            for u in us:
+                pe.matmul(SB[u][:, 0:128], v_of(s, u), T.pts[:, 512 * u + 128 * kp:512 * u + 128 * kp + 128],
+                          kp == 0, kp == G - 1).then_inc(S["o_%d" % u], 1)
 
     pe.wait_ge(S.ld_k, 16)
-    pe.wait_ge(S.cq, 2)
-    pe.wait_ge(S.aq, 2 * len(others))
-    scores(0, True)
-    scores(1, False)
-    pe.wait_ge(S.aqx, len(cable))
-    scores(2, False)
-    scores(3, False)
+    for u in range(4):
+        scores(u)
     pe.wait_ge(S.id, 1)
-    turn(2)
-    turn(3)
-    pe.wait_ge(S.ld_v, 16)
-    for kp, s in enumerate(ko):
-        if s != me:
-            pe.wait_ge(S["av%d" % s], per)
-        for u in (2, 3):
-            if kp == 0:
-                pe.wait_ge(S["c_%d" % u], 1)
-            pv1(u, kp, s)
     turn(0)
     turn(1)
-    for u in (0, 1):
-        pe.wait_ge(S["c_%d" % u], 1)
-        pe.wait_ge(S["fx%d" % u], 1)
-        for kp, s in enumerate(ko):
-            pv1(u, kp, s)
+    turn(2)
+    pe.wait_ge(S.ld_v, 16)
+    pv([0], True)
+    turn(3)
+    pv([1], False)
+    pv([2, 3], True)
+    pe.wait_ge(S.ones, 1)
+    for w in range(4):
+        pe.wait_ge(S["ee%d" % w], HW)
+        pe.matmul(T.cb[:, 128 * w:128 * w + 128], T.ones[:, :], T.ee[:, 128 * w:128 * w + 128], True, True
+                  ).then_inc(S.cbm, 1)
+    pe.wait_ge(S.fx0, 4)
+    for h in range(2):
+        for j in range(2):
+            w = 2 * j + h
+            pe.wait_ge(S["z%d" % w], 1)
+            pe.matmul(Y[h][:, 0:128], T.zz[:, 128 * w:128 * w + 128], T.ident[:, :], j == 0, j == 1
+                      ).then_inc(S["yy%d" % h], 1)
 
     v = g.vector
     v.memset(T.zero[:, :], 0.0).then_inc(S.zero, 1)
-    v.wait_ge(S.ld_q, 16)
-    for i in range(2):
-        h = 2 * me + i
-        v.tensor_copy(T.ql[:, 128 * i + QP * me:128 * i + QP * me + QP], T.qs[:, QP * h:QP * h + QP]).then_inc(S.cq, 1)
+    v.wait_ge(S.aq, 4 * per)
+    for i in (0, 1):
+        for s in range(G):
+            v.tensor_copy(T.ql[:, 128 * i + QP * s:128 * i + QP * s + QP], T.qin[:, s, QP * i:QP * i + QP]
+                          ).then_inc(S["cq%d" % i], 1)
     for u in range(4):
         v.wait_ge(S["s_%d" % u], 4)
-        v.tensor_reduce(shift_col(u), SB[u][:, :], axis=AxisListType.X, op=AluOpType.max, negate=True
+        v.tensor_reduce(T.st[:, u:u + 1], SB[u][:, :], axis=AxisListType.X, op=AluOpType.max, negate=True
                         ).then_inc(S["nm_%d" % u], 1)
 
     def take(u):
         v.wait_ge(S["t_%d" % u], 4)
         v.tensor_copy(T.pts[:, 512 * u:512 * u + 512], PT[u % 2][:, 0:512]).then_inc(S["c_%d" % u], 1)
 
-    take(2)
-    take(3)
-    v.wait_ge(S.o_2, 4)
-    v.tensor_copy(T.xs[:, 0:128], OB[0][:, 0:128]).then_inc(S.fx0, 1)
+    def give(u):
+        v.wait_ge(S["o_%d" % u], 4)
+        for s in range(G):
+            v.tensor_copy(T.xs[:, s, u:128:4], SB[u][:, QP * s:QP * s + QP]).then_inc(S["fx%d" % u], 1)
+
     take(0)
     take(1)
-    v.wait_ge(S.asl, len(eng))
-    v.wait_ge(S.nm_0, 1)
-    v.wait_ge(S.nm_1, 1)
-    v.tensor_tensor(T.dl[:, :], T.sl[:, 0:2], T.st[:, 0:2], AluOpType.subtract).then_inc(S.m1, 1)
+    take(2)
+    give(0)
+    take(3)
+    give(2)
+    v.wait_ge(S.asl, 4 * per)
+    v.tensor_tensor(T.dl[:, :], T.sl[:, 16:32], T.sl[:, 0:16], AluOpType.subtract).then_inc(S.m1, 1)
     v.wait_ge(S.m1, 1)
-    v.tensor_scalar(T.dd[:, 0:2], T.dl[:, :], 0.0, None, AluOpType.min).then_inc(S.m2, 1)
-    v.tensor_scalar(T.dd[:, 2:4], T.dl[:, :], -1.0, 0.0, AluOpType.mult, AluOpType.min).then_inc(S.m2, 1)
+    v.tensor_scalar(T.dd[:, 0:16], T.dl[:, :], 0.0, None, AluOpType.min).then_inc(S.m2, 1)
+    v.tensor_scalar(T.dd[:, 16:32], T.dl[:, :], -1.0, 0.0, AluOpType.mult, AluOpType.min).then_inc(S.m2, 1)
     v.wait_ge(S.m3, 1)
-    v.wait_ge(S.e_0, 1)
-    v.wait_ge(S.e_1, 1)
-    v.tensor_tensor(T.al[:, 0:2], T.aa[:, 0:2], T.st[:, 2:4], AluOpType.mult).then_inc(S.m4, 1)
-    v.tensor_tensor(T.al[:, 2:4], T.aa[:, 2:4], T.sl[:, 2:4], AluOpType.mult).then_inc(S.m4, 1)
-    v.wait_ge(S.m4, 2)
-    v.tensor_tensor(T.den[:, :], T.al[:, 0:2], T.al[:, 2:4], AluOpType.add).then_inc(S.m5, 1)
+    v.tensor_tensor(T.al[:, :], T.aa[:, 0:28], T.sl[:, 4:32], AluOpType.mult).then_inc(S.m4, 1)
+    v.wait_ge(S.m4, 1)
+    v.tensor_tensor(T.den[:, :], T.al[:, 0:12], T.al[:, 16:28], AluOpType.add).then_inc(S.m5, 1)
     v.wait_ge(S.m5, 1)
-    v.reciprocal(T.rc[:, :], T.den[:, :]).then_inc(S.m6, 1)
+    v.tensor_scalar(T.dm[:, :], T.den[:, :], 1.0, None, AluOpType.max).then_inc(S.m6, 1)
     v.wait_ge(S.m6, 1)
-    v.tensor_tensor(T.cc[:, 0:2], T.aa[:, 0:2], T.rc[:, :], AluOpType.mult).then_inc(S.m7, 1)
-    v.tensor_tensor(T.cc[:, 2:4], T.aa[:, 2:4], T.rc[:, :], AluOpType.mult).then_inc(S.m7, 1)
-    v.wait_ge(S.m7, 2)
-    v.wait_ge(S.axl, len(eng))
-    v.tensor_scalar(T.t2[:, 0:128], T.xl[:, 0:128], T.cc[:, 2:3], None, AluOpType.mult).then_inc(S.tt0, 1)
-    for i in range(2):
-        v.wait_ge(S["tt%d" % i], 1)
-        v.wait_ge(S["ow%d" % i], 1)
-        v.tensor_tensor(T.yl[:, 256 * me + 128 * i:256 * me + 128 * i + 128], OB[i][:, 0:128],
-                        T.t2[:, 128 * i:128 * i + 128], AluOpType.add).then_inc(S["fy%d" % i], 1)
+    v.reciprocal(T.rc[:, :], T.dm[:, :]).then_inc(S.m7, 1)
+    v.wait_ge(S.m7, 1)
+    v.tensor_tensor(T.cc[:, 0:12], T.aa[:, 0:12], T.rc[:, :], AluOpType.mult).then_inc(S.m8, 1)
+    v.tensor_tensor(T.cc[:, 16:28], T.aa[:, 16:28], T.rc[:, :], AluOpType.mult).then_inc(S.m8, 1)
+    v.wait_ge(S.m8, 2)
+    v.wait_ge(S.id, 1)
+    for w in (0, 1):
+        for i in range(HW):
+            v.tensor_scalar(e_out(w, i), isel, T.cc[:, 8 * w + i:8 * w + i + 1], None, AluOpType.mult
+                            ).then_inc(S["ee%d" % w], 1)
+    v.wait_ge(S.cbm, 4)
+    for w in (0, 2, 1, 3):
+        v.wait_ge(S["ax%d" % w], per)
+        v.tensor_tensor(T.zz[:, 128 * w:128 * w + 128], T.xl[:, w, :], T.cb[:, 128 * w:128 * w + 128], AluOpType.mult
+                        ).then_inc(S["z%d" % w], 1)
+    v.wait_ge(S.yy0, 2)
+    v.tensor_copy(T.yl[:, 0:128], Y[0][:, 0:128]).then_inc(S.fy0, 1)
 
-    for j in others:
-        g.sync.wait_ge(S["ay%d" % idx[j]], len(eng))
     g.sync.wait_ge(S.fy0, 1)
-    g.sync.wait_ge(S.fy1, 1)
-    g.sync.dma_start(T.y[:, :], T.yl[QP * me:QP * me + QP, :]).then_inc(S.st_y, 16)
-    g.sync.wait_ge(S.st_y, 16)
+    g.sync.dma_start(T.y[:, 0:512], T.yl[:, 0:128]).then_inc(S.st_y0, 16)
+    g.sync.wait_ge(S.st_y0, 16)

from concourse.bass import DstId, RemoteDMATransfer
from concourse.mybir import AluOpType, AxisListType, ActivationFunctionType

N, NH, QP, KP = 8, 8, 32, 128
G = 4
HW = 4

SCRATCH = {
    "qs": ("sbuf", [128, NH * QP], "bfloat16"),
    "ks": ("sbuf", [128, NH * KP], "bfloat16"),
    "vs": ("sbuf", [128, NH * 128], "bfloat16"),
    "qin": ("sbuf", [128, G, HW * QP], "bfloat16"),
    "ql": ("sbuf", [128, HW * 128], "bfloat16"),
    "kl": ("sbuf", [128, G, HW * KP], "bfloat16"),
    "vl": ("sbuf", [128, G, HW * 128], "bfloat16"),
    "zero": ("sbuf", [128, 128], "bfloat16"),
    "ones": ("sbuf", [128, 128], "bfloat16"),
    "ident": ("sbuf", [128, 128], "bfloat16"),
    "p": ("sbuf", [128, 2048], "bfloat16"),
    "pts": ("sbuf", [128, 2048], "bfloat16"),
    "st": ("sbuf", [128, 8], "float32"),
    "sl": ("sbuf", [128, 32], "float32"),
    "xs": ("sbuf", [128, G, 128], "bfloat16"),
    "xl": ("sbuf", [128, G, 128], "bfloat16"),
    "dl": ("sbuf", [128, 16], "float32"),
    "dd": ("sbuf", [128, 32], "float32"),
    "aa": ("sbuf", [128, 32], "float32"),
    "al": ("sbuf", [128, 28], "float32"),
    "den": ("sbuf", [128, 12], "float32"),
    "dm": ("sbuf", [128, 12], "float32"),
    "rc": ("sbuf", [128, 12], "float32"),
    "cc": ("sbuf", [128, 32], "float32"),
    "ee": ("sbuf", [128, 512], "bfloat16"),
    "zz": ("sbuf", [128, 512], "bfloat16"),
    "yl": ("sbuf", [128, 256], "bfloat16"),
    "s0": ("psum", [128, 512], "float32"),
    "s1": ("psum", [128, 512], "float32"),
    "s2": ("psum", [128, 512], "float32"),
    "s3": ("psum", [128, 512], "float32"),
    "pta": ("psum", [128, 1024], "bfloat16"),
    "ptb": ("psum", [128, 1024], "bfloat16"),
    "cb": ("psum", [128, 512], "float32"),
    "ya": ("psum", [128, 512], "float32"),
}

SEMAPHORES = (["ld_q", "ld_k", "ld_v", "snd", "zero", "ones", "id", "aq", "asl", "cbm",
               "m1", "m2", "m3", "m4", "m5", "m6", "m7", "m8"]
              + ["%s%d_%d" % (e, s, hp) for e in ("ak", "av") for s in range(G) for hp in range(2)]
              + ["%s%d" % (e, u) for e in ("cq", "s_", "nm_", "e_", "t_", "c_", "o_", "fx", "ax", "ee", "z") for u in range(4)]
              + ["%s%d" % (e, i) for e in ("yy", "fy", "st_y") for i in range(2)])


def _bits(m):
    return [b for b in range(16) if (m >> b) & 1]


def _mk(bs):
    m = 0
    for b in bs:
        m |= 1 << b
    return m


def _plan(T, topo):
    C = [int(c) for c in T.cores]
    R = range(len(C))
    host = [topo.host(c) for c in C]
    rack = [topo.rack(h) for h in host]
    chip = [topo.chip(c) for c in C]
    chips, racks = sorted(set(chip)), sorted(set(rack))
    half = [chips.index(x) for x in chip]
    slot = [racks.index(rack[j]) * len(chips) + half[j] for j in R]
    near = [[j for j in R if host[j] != host[r] and topo.may_write(C[r], C[j]) and topo.may_write(C[j], C[r])] for r in R]
    grp = [[j for j in R if rack[j] == rack[r]] for r in R]
    kslot = [grp[j].index(j) for j in R]
    return dict(C=C, rack=rack, half=half, slot=slot, near=near, grp=grp, kslot=kslot)


def rank_program(g, core, T, topo):
    r = T.rank_of(core)
    if r is None:
        return
    P = _plan(T, topo)
    C, rack, half, slot, kslot = P["C"], P["rack"], P["half"], P["slot"], P["kslot"]
    me = kslot[r]
    near = P["near"][r]
    others = sorted([j for j in P["grp"][r] if j != r], key=lambda d: (kslot[d] - me) % G)
    S = T.sem
    EXP = ActivationFunctionType.Exp
    CPY = ActivationFunctionType.Copy

    m = 0xFFFF
    for j in others + near:
        m &= topo.mask(core, C[j])
    eng = _bits(m)
    per = len(eng) // 4
    lane = [eng[per * t:per * t + per] for t in range(4)]

    sent = [0]

    def tr(src, dst, d, sem, engs):
        rid, pid = topo.addr(C[d], core)
        sent[0] += len(engs)
        return RemoteDMATransfer(dst_ids=[DstId(rid=rid, pnc=pid)], dma_engine_mask=_mk(engs), remote_sem=sem, srcs=[src],
                                 dsts=[dst], alu_op=0)

    def piece(w, o):
        return (0 if rack[w] == rack[o] else 1) * 2 + half[w]

    def k_of(s, i):
        c = 512 * half[r] + 128 * i
        return T.ks[:, c:c + 128] if s == me else T.kl[:, s, 128 * i:128 * i + 128]

    def v_of(s, i):
        c = 512 * half[r] + 128 * i
        return T.vs[:, c:c + 128] if s == me else T.vl[:, s, 128 * i:128 * i + 128]

    ko = [me] + sorted([s for s in range(G) if s != me], key=lambda s: (me - s) % G)
    SB, PT = [T.s0, T.s1, T.s2, T.s3], [T.pta, T.ptb]
    Y = [T.ya, T.s0]

    g.scalar.dma_start(T.qs[:, :], T.q[:, :]).then_inc(S.ld_q, 16)
    g.sync.dma_start(T.ks[:, :], T.k[:, :]).then_inc(S.ld_k, 16)
    g.sync.dma_start(T.vs[:, :], T.v[:, :]).then_inc(S.ld_v, 16)

    g.wait_ge(S.ld_q, 16)
    g.remote_dma_fused([tr(T.qs[:, 128 * half[w]:128 * half[w] + 128], T.qin[:, slot[r], :], w, S.aq, lane[t])
                        for t, w in enumerate(near)], local_sem=S.snd)
    g.wait_ge(S.ones, 1)
    g.affine_select(T.ident[:, :], T.ones[:, :], [[-1, 128]], AluOpType.is_equal, 0.0, 0, 1).then_inc(S.id, 1)
    seq = [(kind, hp, d) for kind in "kv" for hp in range(2) for d in others]
    g.wait_ge(S.ld_k, 16)
    have_v = False
    for c0 in range(0, len(seq), 4):
        chunk = seq[c0:c0 + 4]
        if not have_v and any(kind == "v" for kind, hp, d in chunk):
            g.wait_ge(S.ld_v, 16)
            have_v = True
        call = []
        for t, (kind, hp, d) in enumerate(chunk):
            c = 512 * half[d] + 256 * hp
            src = T.ks[:, c:c + 256] if kind == "k" else T.vs[:, c:c + 256]
            dst = (T.kl if kind == "k" else T.vl)[:, me, 256 * hp:256 * hp + 256]
            call.append(tr(src, dst, d, S["a%s%d_%d" % (kind, me, hp)], lane[t]))
        g.remote_dma_fused(call, local_sem=S.snd)
    for u in range(4):
        g.wait_ge(S["nm_%d" % u], 1)
        g.wait_ge(S["e_%d" % u], 1)
    g.remote_dma_fused([tr(T.st[:, :], T.sl[:, 8 * piece(r, o):8 * piece(r, o) + 8], o, S.asl, lane[t])
                        for t, o in enumerate(near)], local_sem=S.snd)
    for u in range(4):
        g.wait_ge(S["fx%d" % u], 4)
    g.remote_dma_fused([tr(T.xs[:, slot[o], :], T.xl[:, piece(r, o), :], o, S["ax%d" % piece(r, o)], lane[t])
                        for t, o in enumerate(near)], local_sem=S.snd)
    g.wait_ge(S.snd, sent[0])

    isel = T.ident[:, QP * slot[r]:QP * slot[r] + QP]

    def e_out(w, i):
        return T.ee[:, 128 * w + i:128 * w + 128:4]

    a = g.scalar
    a.wait_ge(S.zero, 1)
    a.activation(T.ones[:, :], T.zero[:, :], EXP).then_inc(S.ones, 1)
    a.wait_ge(S.aq, 4 * per)
    for i in (2, 3):
        for s in range(G):
            a.activation(T.ql[:, 128 * i + QP * s:128 * i + QP * s + QP], T.qin[:, s, QP * i:QP * i + QP], CPY
                         ).then_inc(S["cq%d" % i], 1)
    for u in range(4):
        a.wait_ge(S["nm_%d" % u], 1)
        a.activation(T.p[:, 512 * u:512 * u + 512], SB[u][:, :], EXP, bias=T.st[:, u:u + 1], scale=1.0,
                     accum_out=T.st[:, 4 + u:5 + u]).then_inc(S["e_%d" % u], 1)
    for u in (1, 3):
        a.wait_ge(S["o_%d" % u], 4)
        for s in range(G):
            a.activation(T.xs[:, s, u:128:4], SB[u][:, QP * s:QP * s + QP], CPY).then_inc(S["fx%d" % u], 1)
    a.wait_ge(S.m2, 2)
    a.activation(T.aa[:, :], T.dd[:, :], EXP).then_inc(S.m3, 1)
    a.wait_ge(S.m8, 2)
    a.wait_ge(S.id, 1)
    for w in (2, 3):
        for i in range(HW):
            a.activation(e_out(w, i), isel, CPY, scale=T.cc[:, 8 * w + i:8 * w + i + 1]).then_inc(S["ee%d" % w], 1)
    a.wait_ge(S.yy1, 2)
    a.activation(T.yl[:, 128:256], Y[1][:, 0:128], CPY).then_inc(S.fy1, 1)
    a.wait_ge(S.fy1, 1)
    a.dma_start(T.y[:, 512:1024], T.yl[:, 128:256]).then_inc(S.st_y1, 16)
    a.wait_ge(S.st_y1, 16)

    pe = g.tensor

    def scores(u):
        pe.wait_ge(S["cq%d" % u], 4)
        for kp, s in enumerate(ko):
            if u % 2 == 0 and s != me:
                pe.wait_ge(S["ak%d_%d" % (s, u // 2)], per)
            pe.matmul(SB[u][:, 128 * kp:128 * kp + 128], T.ql[:, 128 * u:128 * u + 128], k_of(s, u),
                      True, True).then_inc(S["s_%d" % u], 1)

    def turn(u):
        pe.wait_ge(S["e_%d" % u], 1)
        if u >= 2:
            pe.wait_ge(S["c_%d" % (u - 2)], 1)
        for kp in range(G):
            pe.transpose(PT[u % 2][:, 128 * kp:128 * kp + 128], T.p[:, 512 * u + 128 * kp:512 * u + 128 * kp + 128],
                         T.ident[:, :]).then_inc(S["t_%d" % u], 1)

    def pv(us, first):
        for u in us:
            pe.wait_ge(S["c_%d" % u], 1)
        for kp, s in enumerate(ko):
            if first and s != me:
                pe.wait_ge(S["av%d_%d" % (s, us[0] // 2)], per)
            for u in us:
                pe.matmul(SB[u][:, 0:128], v_of(s, u), T.pts[:, 512 * u + 128 * kp:512 * u + 128 * kp + 128],
                          kp == 0, kp == G - 1).then_inc(S["o_%d" % u], 1)

    pe.wait_ge(S.ld_k, 16)
    for u in range(4):
        scores(u)
    pe.wait_ge(S.id, 1)
    turn(0)
    turn(1)
    turn(2)
    pe.wait_ge(S.ld_v, 16)
    pv([0], True)
    turn(3)
    pv([1], False)
    pv([2, 3], True)
    pe.wait_ge(S.ones, 1)
    for w in range(4):
        pe.wait_ge(S["ee%d" % w], HW)
        pe.matmul(T.cb[:, 128 * w:128 * w + 128], T.ones[:, :], T.ee[:, 128 * w:128 * w + 128], True, True
                  ).then_inc(S.cbm, 1)
    pe.wait_ge(S.fx0, 4)
    for h in range(2):
        for j in range(2):
            w = 2 * j + h
            pe.wait_ge(S["z%d" % w], 1)
            pe.matmul(Y[h][:, 0:128], T.zz[:, 128 * w:128 * w + 128], T.ident[:, :], j == 0, j == 1
                      ).then_inc(S["yy%d" % h], 1)

    v = g.vector
    v.memset(T.zero[:, :], 0.0).then_inc(S.zero, 1)
    v.wait_ge(S.aq, 4 * per)
    for i in (0, 1):
        for s in range(G):
            v.tensor_copy(T.ql[:, 128 * i + QP * s:128 * i + QP * s + QP], T.qin[:, s, QP * i:QP * i + QP]
                          ).then_inc(S["cq%d" % i], 1)
    for u in range(4):
        v.wait_ge(S["s_%d" % u], 4)
        v.tensor_reduce(T.st[:, u:u + 1], SB[u][:, :], axis=AxisListType.X, op=AluOpType.max, negate=True
                        ).then_inc(S["nm_%d" % u], 1)

    def take(u):
        v.wait_ge(S["t_%d" % u], 4)
        v.tensor_copy(T.pts[:, 512 * u:512 * u + 512], PT[u % 2][:, 0:512]).then_inc(S["c_%d" % u], 1)

    def give(u):
        v.wait_ge(S["o_%d" % u], 4)
        for s in range(G):
            v.tensor_copy(T.xs[:, s, u:128:4], SB[u][:, QP * s:QP * s + QP]).then_inc(S["fx%d" % u], 1)

    take(0)
    take(1)
    take(2)
    give(0)
    take(3)
    give(2)
    v.wait_ge(S.asl, 4 * per)
    v.tensor_tensor(T.dl[:, :], T.sl[:, 16:32], T.sl[:, 0:16], AluOpType.subtract).then_inc(S.m1, 1)
    v.wait_ge(S.m1, 1)
    v.tensor_scalar(T.dd[:, 0:16], T.dl[:, :], 0.0, None, AluOpType.min).then_inc(S.m2, 1)
    v.tensor_scalar(T.dd[:, 16:32], T.dl[:, :], -1.0, 0.0, AluOpType.mult, AluOpType.min).then_inc(S.m2, 1)
    v.wait_ge(S.m3, 1)
    v.tensor_tensor(T.al[:, :], T.aa[:, 0:28], T.sl[:, 4:32], AluOpType.mult).then_inc(S.m4, 1)
    v.wait_ge(S.m4, 1)
    v.tensor_tensor(T.den[:, :], T.al[:, 0:12], T.al[:, 16:28], AluOpType.add).then_inc(S.m5, 1)
    v.wait_ge(S.m5, 1)
    v.tensor_scalar(T.dm[:, :], T.den[:, :], 1.0, None, AluOpType.max).then_inc(S.m6, 1)
    v.wait_ge(S.m6, 1)
    v.reciprocal(T.rc[:, :], T.dm[:, :]).then_inc(S.m7, 1)
    v.wait_ge(S.m7, 1)
    v.tensor_tensor(T.cc[:, 0:12], T.aa[:, 0:12], T.rc[:, :], AluOpType.mult).then_inc(S.m8, 1)
    v.tensor_tensor(T.cc[:, 16:28], T.aa[:, 16:28], T.rc[:, :], AluOpType.mult).then_inc(S.m8, 1)
    v.wait_ge(S.m8, 2)
    v.wait_ge(S.id, 1)
    for w in (0, 1):
        for i in range(HW):
            v.tensor_scalar(e_out(w, i), isel, T.cc[:, 8 * w + i:8 * w + i + 1], None, AluOpType.mult
                            ).then_inc(S["ee%d" % w], 1)
    v.wait_ge(S.cbm, 4)
    for w in (0, 2, 1, 3):
        v.wait_ge(S["ax%d" % w], per)
        v.tensor_tensor(T.zz[:, 128 * w:128 * w + 128], T.xl[:, w, :], T.cb[:, 128 * w:128 * w + 128], AluOpType.mult
                        ).then_inc(S["z%d" % w], 1)
    v.wait_ge(S.yy0, 2)
    v.tensor_copy(T.yl[:, 0:128], Y[0][:, 0:128]).then_inc(S.fy0, 1)

    g.sync.wait_ge(S.fy0, 1)
    g.sync.dma_start(T.y[:, 0:512], T.yl[:, 0:128]).then_inc(S.st_y0, 16)
    g.sync.wait_ge(S.st_y0, 16)
